import numpy as np, ml_dtypes
CORES = [16,18,20,22]
N = 4
BF = ml_dtypes.bfloat16
def gentries(a):
    return np.ascontiguousarray(a.reshape(8, 16, -1).transpose(0, 2, 1)).reshape(8, -1)
def gtable(e):
    e = np.asarray(e); return np.ascontiguousarray(e.reshape(8, -1, 16).transpose(0, 2, 1)).reshape(128, -1).astype(np.int32)
G, C, P, RO, YC = 128, 32, 64, 3, 32
W, LG, LC, H, M = 4096, 7, 5, 64, 32
BIG = 2 ** 24
def probes(u, k):
    return (((u * u) >> 5)[..., None] + u[..., None] * k) & (W - 1)
def base(rng):
    ring = rng.integers(0, 256, (8, 8, 64, 16)); a = rng.integers(0, 8, (N, 8, G, 1)); b = rng.integers(0, 64, (N, 8, G, 1))
    X = ring[np.arange(8)[None, :, None, None], a, (b + np.arange(C)) & 63]
    X = np.clip(X + rng.integers(-4, 5, X.shape), 0, 255)
    th = np.where(rng.random((N, 8, P)) < 0.25, rng.integers(0, 300, (N, 8, P)), rng.integers(600, 1600, (N, 8, P)))
    return X, rng.integers(1, 256, (N, 8, 16)), rng.integers(0, 2048, (N, 8, RO, P)), th
def pack(X, wt, km, th):
    X = np.ascontiguousarray(X.reshape(N, 8, G, C, 16).transpose(0, 1, 4, 2, 3)).reshape(N, 128, W)
    return {"gen0": X.astype(np.float32).astype(BF), "wt": np.ascontiguousarray(wt.reshape(N, 128, 1)).astype(np.int32),
            "km": np.stack([gtable(a.reshape(8, -1)) for a in km]), "th": np.stack([gtable(a) for a in th])}
def setup_inputs(rng):
    return pack(*base(rng))
def column(rng, w, u):
    x = rng.integers(0, 256, 16); r = (int(u) - int(np.sum(w[2:] * x[2:]))) & (W - 1); x[0] = r & 15; x[1] = r >> 4
    return x
def link(rng, Y, w, k, o, alone=False):
    c = probes(np.arange(W)[None, :], k[None, None, :])[0]
    od = np.argsort(c.reshape(-1).astype(np.int16), kind="stable"); st = np.searchsorted(c.reshape(-1)[od], np.arange(W + 1))
    for i in range(G - 1):
        if alone and i == 1: continue
        j = 2 if alone and i == 0 else i + 1
        t = C * j + int(o[i]); us = od[st[t]:st[t + 1]] // P; us = us[~np.any(c[us] == C * i + C - 1, axis=1)]
        if len(us):
            x = column(rng, w, us[int(rng.integers(0, len(us)))]); Y[i, C - 1] = x; Y[j, int(o[i])] = x
def setup_inputs_deep(rng):
    X, wt, km, th = base(rng); th = rng.integers(30, 41, th.shape); B = 8 * N; b = np.arange(B)
    X = X.reshape(B, G, C, 16); w = wt.reshape(B, 1, 16).astype(np.int32); k0 = km[:, :, 0].reshape(B, 1, P).astype(np.int32); tries = min(128, max(16, 16 * G // P))
    for i in range(G - 1):
        x = rng.integers(0, 256, (B, tries, 16), dtype=np.int32); u = (np.sum(w * x, axis=2) & (W - 1)).astype(np.int32)
        c = probes(u, k0); o = c & (C - 1); to = np.where((b % 4 == 2) & (i == 0), 2, i + 1)
        hit = ((c >> LC) == to[:, None, None]) & (o != C - 1) & ~np.any(c == C * i + C - 1, axis=2)[..., None]
        like = np.where((b % 4 == 0)[:, None, None], o, np.where((b % 4 == 2)[:, None, None], C - 1 - o, 0)) + 1
        s = np.where(hit, like, 0).reshape(B, -1); a = np.argmax(s, axis=1)
        do = (s[b, a] > 0) & ((b % 2 == 0) | (rng.random(B) < 0.9)) & ((b % 4 != 2) | (i != 1))
        bb = b[do]; aa = a[do]; xs = x[bb, aa // P]
        X[bb, i, C - 1] = xs; X[bb, to[bb], o.reshape(B, -1)[bb, aa]] = xs
    X = X.reshape(N, 8, G, C, 16)
    for g in (3, 4, 7):
        wt[:, g, 0] = 1; wt[:, g, 1] = 16
    for r in range(N): link(rng, X[r, 4], wt[r, 4], km[r, 4, 0], np.full(G, C - 2))
    k = np.arange(2048)
    for g in (3, 7):
        h = int(rng.choice(np.array([3, 5, 7, 9]))); q0 = int(np.argmin((np.arange(C) * h + 1) & (C - 1))); Y = X[:, g].copy()
        for r in range(N):
            u = h - 1 + H * int(rng.integers(0, W // H)); c = (u * u // 32 + k * u) & (W - 1)
            km[r, g, 0] = rng.choice(k[(c & (C - 1)) != C - 1], P); Y[:, r * M:(r + 1) * M, q0] = column(rng, wt[r, g], u)
        for d in range(N): link(rng, Y[d], wt[d, g], km[d, g, 1], np.full(G, C - 2) if g == 3 else 2 * rng.integers(0, C // 2, G), g == 7)
        p = (C * np.arange(G)[:, None] + h * np.arange(C)) & (W - 1)
        for r in range(N):
            kid = np.zeros((G, C, 16), np.int64)
            for d in range(N): kid[(d - r) % N::N] = Y[d, r * M:(r + 1) * M]
            X[r, g, p >> LC, p & (C - 1)] = kid
    return pack(X, wt, km, th)
def setup_inputs_edges(rng):
    X, wt, km, th = base(rng)
    th[:, 0] = 0; e = X[:, 0, :1, C - 1].copy(); X[:, 0, ::2, C - 1] = e; X[:, 0, :, ::4] = e[:, :, None]
    f = rng.integers(0, 16, (N, G, C, 1)); X[:, 1] = (np.arange(16) == f) & (rng.random((N, G, C, 1)) < 0.2); X[:, 1, :, C - 1] = 255; th[:, 1] = 4080
    k = np.arange(2048)
    for q in range(N):
        u = int(255 * np.sum(wt[q, 1])) & (W - 1); c = ((u * u >> 5) + k * u) & (W - 1)
        good = k[(c & (C - 1)) != C - 1]
        km[q, 1, 0] = rng.choice(good if len(good) else k, P)
    km[:, 2] = rng.choice(np.array([0, 1, 3, 2047]), (N, RO, P))
    X[:, 3, ::2, C - 1] = 0; X[:, 3, 0, 0] = 0
    wt[:, 4] = 255; X[:, 4] = 255 - rng.integers(0, 3, (N, G, C, 16))
    X[:, 5, :, C - 1] = rng.integers(0, 256, (N, 1, 16))
    X[:, 6] = 255 * rng.integers(0, 2, (N, G, C, 16)); th[:, 6] = 255 * rng.integers(2, 9, (N, P))
    return pack(X, wt, km, th)
def setup_inputs_far(rng):
    X, wt, km, th = base(rng); k = np.arange(2048)
    for q in range(N):
        for g in (0, 1, 2, 4, 5):
            wt[q, g, 0] |= 1; wt[q, g, 8:] = wt[q, g, :8]
            b = np.concatenate([rng.integers(110, 181, (256, 8)), rng.integers(80, 101, (256, 8))], axis=1); u = np.sum(wt[q, g] * b, axis=1) & (W - 1)
            c = probes(u[None, :], k[None, None, :])[0]
            ok = (c == W - 1) if g == 4 else (c >= 3 * W // 4) & ((c & (C - 1)) != C - 1)
            if g == 5: ok = ok & np.any(c == 0, axis=1)[:, None]
            a, m = np.nonzero(ok); s = int(rng.integers(0, len(a))); x = b[a[s]]; c = c[a[s]]; K = int(m[s]); j = int(c[K]) >> LC; o = int(c[K]) & (C - 1)
            e = rng.integers(35, 71, (G, 8)); e[G // 4:G // 2] = rng.integers(0, 35, (G // 2 - G // 4, 8))
            if g > 2: e[:] = 0
            last = x + np.concatenate([e, -e], axis=1); X[q, g, :, C - 1] = last; km[q, g, 0] = K
            if g == 1:
                km[q, 1, 0] = rng.choice(k[(c & (C - 1)) != C - 1], P); th[q, 1] = rng.integers(2048, 4081, P)
                X[q, 1, :, :C - 1, :8] = rng.integers(0, 41, (G, C - 1, 8)); X[q, 1, :, :C - 1, 8:] = rng.integers(215, 256, (G, C - 1, 8))
            elif g == 4:
                d = rng.integers(1, 60, 16); X[q, 4, G - 1, C - 1] = x - d; th[q, 4] = int(np.sum(d)) + 1
            elif g == 5:
                d = rng.integers(1, 30, 16); X[q, 5, 0, 0] = x - d; X[q, 5, j, o] = x - rng.integers(30, 60, 16)
                km[q, 5, 0, ::2] = int(np.argmax(c == 0)); th[q, 5] = 4080; th[q, 5, ::2] = int(np.sum(d))
            else:
                v = np.repeat(np.array([0, 255]), 8); X[q, g, j, o] = v
                th[q, g] = 4080 if g == 0 else int(np.min(np.sum(np.abs(last - v), axis=1)))
    X[:, 3] = 255 - rng.integers(0, 64, (N, G, C, 16)); X[:, 3, :, C - 1] = rng.integers(0, 64, (N, G, 16)); th[:, 3] = rng.integers(2048, 4081, (N, P))
    return pack(X, wt, km, th)
def setup_inputs_spread(rng):
    X, wt, km, th = base(rng)
    X = np.minimum((rng.random((N, 8, G, C, 16)) * np.exp2(rng.integers(0, 9, (N, 8, G, C, 1)))).astype(np.int64), 255)
    wt = np.clip(np.exp2(8 * rng.random(wt.shape)).astype(np.int64), 1, 255); km = np.clip(np.exp2(11 * rng.random(km.shape)).astype(np.int64) - 1, 0, 2047); km[..., ::2] = rng.integers(0, 2048, km[..., ::2].shape)
    th = rng.integers(0, 4081, th.shape)
    return pack(X, wt, km, th)
def setup_inputs_ties(rng):
    X, wt, km, th = base(rng)
    pat = rng.integers(1, 254, (8, 4, 16)); a = rng.integers(0, 4, (N, 8, G, C))
    X = pat[np.arange(8)[None, :, None, None], a] + rng.integers(0, 2, (N, 8, G, C, 16)); th = rng.integers(3, 11, th.shape)
    return pack(X, wt, km, th)
def check_inputs(d):
    bad = []; v = np.asarray(d["gen0"]).astype(np.float32)
    if not np.all((v >= 0) & (v <= 255) & (v == np.floor(v))): bad.append("gen0 holds other numbers than 0 .. 255")
    for k, lo, hi in (("wt", 1, 255), ("km", 0, 2047), ("th", 0, 4080)):
        if np.min(d[k]) < lo or np.max(d[k]) > hi: bad.append("range of " + k)
    return bad
def reference(gen0, wt, km, th):
    B = 8 * N; X = gen0.astype(np.float32).astype(np.int32).reshape(B, 16, W); w = wt.astype(np.int64).reshape(B, 16, 1)
    kl = np.stack([gentries(a) for a in km]).astype(np.int64).reshape(B, RO, P); tl = np.stack([gentries(a) for a in th]).astype(np.int64).reshape(B, 1, P)
    ar = np.arange(G); q = np.arange(C); rows = np.arange(B)[:, None]
    for t in range(RO):
        x = X[:, :, C - 1::C]
        u = np.sum(w * x, axis=1) & (W - 1)
        c = probes(u, kl[:, t][:, None, :])
        pr = np.take_along_axis(X, c.reshape(B, 1, G * P), 2).reshape(B, 16, G, P)
        D = np.sum(np.abs(pr - x[..., None]), axis=1).astype(np.int64)
        best = np.min(np.where(D < tl, D * W + c, BIG), axis=2)
        j = (best & (W - 1)) >> LC; o = best & (C - 1); ok = (best < BIG) & (j > ar)
        acc = np.full((B, G), BIG, np.int64)
        np.minimum.at(acc, (rows, np.where(ok, j, 0)), np.where(ok, (best - (best & (W - 1))) + ar * C + o, BIG))
        got = acc < BIG; cut = np.where(got, 1 + ((acc & (C - 1)) >> 1), 0); ln = C - cut
        root = np.where(got, (acc & (W - 1)) >> LC, ar)
        for _ in range(LG): root = np.take_along_axis(root, root, 1)
        od = np.argsort(root * G + ar, axis=1)
        ls = np.take_along_axis(ln, od, 1); pos = np.zeros((B, G), np.int64)
        np.put_along_axis(pos, od, np.add.accumulate(ls, axis=1) - ls, 1); L = np.sum(ln, axis=1)
        place = np.where(q < cut[..., None], W, pos[..., None] + q - cut[..., None])
        src = np.zeros((B, W + 1), np.int64); np.put_along_axis(src, place.reshape(B, W), np.arange(W)[None, :], 1)
        p = ((ar * L[:, None]) >> LG)[..., None] + q * (1 + (u & (H - 1)))[..., None]
        p = np.where(p >= L[:, None, None], p - L[:, None, None], p)
        col = np.take_along_axis(src, p.reshape(B, W), 1)
        kid = np.take_along_axis(X, col[:, None, :], 2).reshape(N, 8, 16, G, C); nxt = np.empty_like(kid)
        for r in range(N):
            for d in range(N): nxt[d, :, :, r * M:(r + 1) * M] = kid[r, :, :, (d - r) % N::N]
        X = nxt.reshape(B, 16, W)
    return {"y": np.ascontiguousarray(X.reshape(N, 128, G, C)[..., :YC]).reshape(N, 128, G * YC).astype(np.float32).astype(BF)}

@@ -1,0 +1,492 @@
+from concourse.bass import DstId, RemoteDMATransfer
+from concourse.mybir import AluOpType, AxisListType, ActivationFunctionType
+
+A = AluOpType
+F = ActivationFunctionType
+N = 4
+MB = 1024
+BANKS = (("b2", (7, 6)), ("b3", (5, 4)), ("b4", (3, 2, 1, 0)))
+SEG = {}
+for _bank, _js in BANKS:
+    _c = 0
+    for _j in _js:
+        SEG[_j] = (_bank, _c, 16 * (_j + 1))
+        _c += 16 * (_j + 1)
+BANKW = {"b2": 240, "b3": 176, "b4": 160}
+CTO = {"b2": 0, "b3": 240, "b4": 416}
+SCH = [(0, 8), (8, 16)]
+VCH = [(16, 24), (24, 32), (32, 40), (40, 48), (48, 56), (56, 60), (60, 64)]
+LATE = 56
+LAYS = 136
+
+_f, _h, _b, _i, _u = "float32", "float16", "bfloat16", "int32", "uint16"
+_sb = {
+    _b: "x0:4096 x1:4096 x2:4096 x3:4096 lay:4096 ko0:3072 ko1:3072 ko2:3072 lr0:512 lr1:512 q16:128 q17:128 bq:128 "
+        "bo:128 bo27:128 mk2:256 idb:128 nid:128 ld:2048 bw:128 ones:128 omi:128 gsel:1024 grp:1024 jt:512 kcol:8 "
+        "rst:128 xrep:1024 ga:2048 d:8192 ab:8192 gd:512 ej:128 ef:128 el:128 mm:128 lb:1024 cmp:1024 "
+        "f0:128 f1:128 f2:128 f3:128 f4:128 f7:128 h0:128 h1:128 h2:128 h3:128",
+    _h: "bo12:128 boh:128 idh:128 c16:512 ed:256",
+    _f: "wtf:1 ekt:256 kr:192 th2:512 pf:1 pm:1 pm16:1 pm4:1 pg:1 row:128 mg:128 bof:128 idf:128 i16:8 i1:8 gc:8 "
+        "pgc:8 negr:8 jtf:512 kc:512 il:8 eq0:8 tgt:8 tc:8 ct:576 self:8 ioc:8 pl:256 kperm:128 ac:128 uf:8 u2:8 "
+        "h31:8 w31:8 q31:8 mk:512 bf:8 jm:8 accf:8 sc:128 lc:1 pp:256 pw:256 mp:128 t4:128 vrow:128 sp:128 wb:264 "
+        "w1:256 ff:256",
+    _i: "wti:1 kt:16 pi:1 pmi:1 pgi:1 expi:16 ui:8 ub:8 sq:8 s5:8 cv:512 ci:512 best:8 jI:8 oI:8 jv:8 dio:16 "
+        "acc:8 fI:8 cI:8 lI:8 hI:128 h63:128 kl:128 sk:128 hb:8 k31:8 s31:8 p31:8 cell:8 si:256 sj:256",
+    _u: "expl:16 cl:512 plist:256 celll:8 l31:8 sl:256 fl0:8 fl1:8 fl2:8 fl3:8 fl4:8",
+}
+WIDTH, TYPE, PLACE, SCRATCH, _used = {}, {}, {}, {}, {}
+for _t, _list in _sb.items():
+    for _e in _list.split():
+        _k, _w = _e.split(":")
+        WIDTH[_k], TYPE[_k], PLACE[_k] = int(_w), _t, (_k, 0)
+        if int(_w) <= 16 and _k not in ("wti", "kt"):
+            PLACE[_k] = ("small_" + _t, _used.get(_t, 0))
+            _used[_t] = _used.get(_t, 0) + 16
+        else:
+            SCRATCH[_k] = ("sbuf", [128, int(_w)], _t)
+for _k, _v in _used.items():
+    SCRATCH["small_" + _k] = ("sbuf", [128, _v], _k)
+for _k in range(8):
+    SCRATCH["b%d" % _k] = ("psum", [128, 512], _f)
+    WIDTH["b%d" % _k], TYPE["b%d" % _k], PLACE["b%d" % _k] = 512, _f, ("b%d" % _k, 0)
+SEMAPHORES = ["qV", "qS", "qP", "qG"] + ["dl%d" % k for k in range(12)] + \
+    ["ar%d_%d" % (t, k) for t in range(3) for k in range(4)] + ["%s%d" % (s, t) for t in range(3) for s in ("ls", "lq", "sm")]
+
+
+def build_tracker(g, T):
+    eng = {"V": g.vector, "S": g.scalar, "P": g.tensor, "G": g, "Y": g.sync}
+    cnt = {"V": 0, "S": 0, "P": 0, "G": 0}
+    clk = {q: {} for q in eng}
+    snap = {}
+    acc = {}
+    ndma = [0]
+
+    def meet(r, e):
+        if r[1] >= e[3] or e[2] >= r[2]:
+            return False
+        return not (r[3] == e[4] and r[3] > 1 and (r[1] - e[2]) % r[3])
+
+    def sync(q, outs, ins):
+        need = {}
+        for w, regs in ((True, outs), (False, ins)):
+            for r in regs:
+                psum = SCRATCH[r[0]][0] == "psum"
+                for e in acc.get(r[0], ()):
+                    hit = (psum and e[0] != q) or ((w or e[5]) and (q, e[0]) != ("P", "P") and meet(r, e))
+                    tok = e[1]
+                    if hit and clk[q].get(tok[0], 0) < tok[1] and need.get(tok[0], 0) < tok[1]:
+                        need[tok[0]] = tok[1]
+        items = sorted(need.items(), key=lambda kv: kv[0])
+        for s, v in items:
+            if not any(s2 != s and snap[(s2, v2)].get(s, 0) >= v for s2, v2 in items):
+                eng[q].wait_ge(T.sem[s], v)
+        for tok in items:
+            for s, v in snap[tok].items():
+                clk[q][s] = max(v, clk[q].get(s, 0))
+
+    def note(q, tok, outs, ins):
+        for w, regs in ((True, outs), (False, ins)):
+            for r in regs:
+                lst = acc.setdefault(r[0], [])
+                lst[:] = [e for e in lst if not (e[0] == q and (e[5] == w or w) and e[2] >= r[1] and e[3] <= r[2]
+                                                 and (r[3] == 1 or (e[4] == r[3] and (e[2] - r[1]) % r[3] == 0)))]
+                lst.append((q, tok, r[1], r[2], r[3], w))
+
+    def done(q, who, tok, outs, ins):
+        snap[tok] = dict(clk[q]) if q else {}
+        snap[tok][tok[0]] = tok[1]
+        note(who, tok, outs, ins)
+
+    def emit(q, call, outs, ins):
+        sync(q, outs, ins)
+        cnt[q] += 1
+        call(eng[q]).then_inc(T.sem["q" + q], 1)
+        done(q, q, ("q" + q, cnt[q]), outs, ins)
+
+    def dma(q, out_ap, in_ap, outs, ins):
+        sync(q, outs, ins)
+        s = "dl%d" % ndma[0]
+        ndma[0] += 1
+        eng[q].dma_start(out_ap, in_ap).then_inc(T.sem[s], 16)
+        done(q, s, (s, 16), outs, ins)
+
+    def arrive(s, val, outs):
+        done(None, s, (s, val), outs, ())
+
+    def finish(extra):
+        for q in ("V", "S", "P", "G"):
+            g.wait_ge(T.sem["q" + q], cnt[q])
+        for k in range(ndma[0]):
+            g.wait_ge(T.sem["dl%d" % k], 16)
+        for s, v in extra:
+            g.wait_ge(T.sem[s], v)
+    return emit, dma, sync, arrive, finish
+
+
+def rank_program(g, core, T, topo):
+    rank = T.rank_of(core)
+    if rank is None:
+        return
+    emit, dma, sync, arrive, finish = build_tracker(g, T)
+
+    def R(name, a=0, b=None, st=1):
+        p, o = PLACE[name]
+        return (p, o + a, o + (WIDTH[name] if b is None else b), st)
+
+    def blk(name, k, w=128):
+        return R(name, w * k, w * k + w)
+
+    def ap(r):
+        if r[3] == 1:
+            return T[r[0]][:, r[1]:r[2]]
+        return T[r[0]][:, r[1]:r[2]:r[3]]
+
+    def src(r, idx):
+        return ap(r) if idx is None else ap(r).indirect(ap(idx))
+
+    def regs(*rs):
+        return [r for r in rs if isinstance(r, tuple)]
+
+    def sca(v):
+        return ap(v) if isinstance(v, tuple) else v
+
+    def tt(out, in0, in1, op, idx=None):
+        emit("V", lambda e: e.tensor_tensor(ap(out), src(in0, idx), ap(in1), op), [out], regs(in0, in1, idx))
+
+    def ts(out, in0, s1, s2, op0, op1=None):
+        if op1 is None:
+            emit("V", lambda e: e.tensor_scalar(ap(out), ap(in0), sca(s1), None, op0), [out], regs(in0, s1))
+        else:
+            emit("V", lambda e: e.tensor_scalar(ap(out), ap(in0), sca(s1), sca(s2), op0, op1), [out], regs(in0, s1, s2))
+
+    def cp(out, in_, idx=None, oidx=None):
+        emit("V", lambda e: e.tensor_copy(src(out, oidx), src(in_, idx)), [out], regs(in_, idx, oidx))
+
+    def fill(out, v):
+        emit("V", lambda e: e.memset(ap(out), v), [out], [])
+
+    def red(out, in_, op, absv=False):
+        emit("V", lambda e: e.tensor_reduce(ap(out), ap(in_), AxisListType.X, op, apply_absolute_value=absv), [out], [in_])
+
+    def scan(out, d0, d1, init, op0, op1):
+        emit("V", lambda e: e.tensor_tensor_scan(ap(out), ap(d0), ap(d1), sca(init), op0, op1), [out], regs(d0, d1, init))
+
+    def act(out, in_, fn, idx=None, scale=None, bias=None):
+        kw = {}
+        if scale is not None:
+            kw["scale"] = sca(scale)
+        if bias is not None:
+            kw["bias"] = sca(bias)
+        emit("S", lambda e: e.activation(ap(out), src(in_, idx), fn, **kw), [out], regs(in_, idx, scale, bias))
+
+    def mm(out, lhsT, rhs, start, stop):
+        emit("P", lambda e: e.matmul(ap(out), ap(lhsT), ap(rhs), start, stop), [out], [lhsT, rhs])
+
+    def iota(name, pattern, cm=0):
+        out = R(name)
+        kw = {} if TYPE[name] == _i else {"allow_small_or_imprecise_dtypes": True}
+        emit("G", lambda e: e.iota(ap(out), pattern, 0, cm, **kw), [out], [])
+
+    dma("Y", T.x0[:], T.gen0[:], [R("x0")], [])
+    dma("S", T.kt[:, 0:12], T.km[:], [R("kt", 0, 12)], [])
+    dma("S", T.kt[:, 12:16], T.th[:], [R("kt", 12, 16)], [])
+    dma("S", T.wti[:], T.wt[:], [R("wti")], [])
+
+    iota("pi", [[0, 1]], 1)
+    iota("q16", [[0, 8], [1, 16]])
+    iota("mg", [[1, 8], [0, 16]])
+    iota("expi", [[1, 16]])
+    iota("row", [[1, 128]])
+    iota("i16", [[16, 8]])
+    iota("i1", [[1, 8]])
+    iota("kperm", [[1, 4], [4, 32]])
+    iota("jtf", [[0, 4], [1, 128]])
+    iota("pl", [[16, 256]])
+    MK = R("mk2", 0, 128)
+    E8 = R("expl", 0, 8)
+    cp(R("pf"), R("pi"))
+    ts(R("pmi"), R("pi"), 15, None, A.bitwise_and)
+    ts(R("pgi"), R("pi"), 4, None, A.arith_shift_right)
+    cp(R("expl"), R("expi"))
+    cp(R("pm"), R("pmi"))
+    cp(R("pg"), R("pgi"))
+    ts(R("q17"), R("q16"), 1.0, None, A.add)
+    ts(R("bo"), R("mg"), R("pg"), None, A.is_equal)
+    ts(R("bof"), R("mg"), R("pg"), None, A.is_equal)
+    ts(MK, R("q16"), R("pm"), None, A.is_equal)
+    ts(R("mk2", 128, 256), R("q16"), R("pm"), None, A.is_equal)
+    tt(R("bq"), R("q17"), R("bo"), A.mult)
+    for s in range(16):
+        ts(blk("ld", s), R("bq"), float(s + 1), 4096.0, A.is_equal, A.mult)
+    cp(R("wtf"), R("wti"))
+    ts(R("bw"), R("bo"), R("wtf"), None, A.mult)
+    tt(R("ekt"), R("kt"), R("mk2"), A.mult, R("expl"))
+    mm(R("b1", 0, 256), R("bof"), R("ekt"), True, True)
+    ts(R("idf"), R("row"), R("pf"), None, A.is_equal)
+    ts(R("idb"), R("row"), R("pf"), None, A.is_equal)
+    ts(R("nid"), R("row"), R("pf"), -1.0, A.is_equal, A.mult)
+    ts(R("idh"), R("row"), R("pf"), None, A.is_equal)
+    ts(R("rst"), R("q16"), 0.0, None, A.is_gt)
+    fill(R("ones"), 1.0)
+    ts(R("il"), R("i16"), R("pm"), None, A.add)
+    ts(R("pgc"), R("i1"), R("pg"), None, A.is_equal)
+    ts(R("gc"), R("i16"), R("pf"), 128.0, A.is_equal, A.mult)
+    ts(R("eq0"), R("il"), 0.0, None, A.is_equal)
+    ts(R("pm16"), R("pm"), 16.0, None, A.add)
+    ts(R("pm4"), R("pm"), 4095.0, 4095.0, A.mult, A.add)
+    tt(R("tgt"), R("il"), R("eq0"), A.subtract)
+    ts(R("pgc", 4, 8), R("pgc", 4, 8), 0.5, None, A.mult)
+    ts(R("self"), R("il"), 32.0, 4095.0 * 4096.0, A.mult, A.add)
+    ts(R("tc"), R("tgt"), -(2.0 ** 27), 2.0 ** 23 + 2048.0, A.mult, A.add)
+    ts(R("ioc"), R("il"), 32.0, 1.0 - 2048.0, A.mult, A.add)
+    ts(R("kcol"), R("ones", 0, 8), R("pf"), None, A.mult)
+    ts(R("omi"), R("row"), R("pf"), None, A.not_equal)
+    act(R("bo27"), R("bo"), F.Copy, None, 2.0 ** 27)
+    act(R("bo12"), R("bo"), F.Copy, None, 4096.0)
+    act(R("boh"), R("bo"), F.Copy)
+    act(R("kc"), R("jtf"), F.Identity, None, 0.0, 2048.0 - 2.0 ** 24)
+    act(R("kr"), R("b1", 0, 192), F.Copy)
+    for k in range(8):
+        act(R("th2", k, 512, 8), R("b1", 192, 256), F.Identity, None, 4096.0, -(2.0 ** 24))
+    act(R("b1", 256, 512), R("pl"), F.Identity, None, None, R("pm"))
+    act(R("b1", 0, 256), R("pl"), F.Identity, None, 4095.0, R("pm4"))
+
+    def later_constants():
+        for k in range(8):
+            act(blk("grp", k), R("bo"), F.Copy, None, R("pgc", k, k + 1))
+        act(R("jt"), R("jtf"), F.Copy, None, 1.0 / 128.0)
+        act(R("ac"), R("row"), F.Identity, None, 32.0, 32.0)
+        for k in range(8):
+            act(blk("gsel", k), R("ones"), F.Copy, None, R("gc", k, k + 1))
+    extra = []
+    ne = len(topo.engines(core, T.cores[(rank + 1) % N]))
+    far = [kr for kr in (1, 2, 3) if topo.die(T.cores[(kr + rank) % N]) != topo.die(core)]
+    near = [kr for kr in (1, 2, 3) if kr not in far]
+
+    for t in range(3):
+        X = "x%d" % t
+        Xn = "x%d" % (t + 1)
+        ko = "ko%d" % t
+        for r in range(N):
+            if t:
+                last = R("lr%d" % (t - 1), 128 * r + (rank - r) % N, 128 * r + 128, 4)
+            else:
+                last = R(X, MB * r + 31, MB * r + MB, 32)
+            mm(blk("b4", r, 32), R("bw"), last, True, True)
+            act(blk("xrep", r, 32), last, F.Copy)
+        mm(R("b0"), R("idf"), R("kc"), True, False)
+        for k in range(4):
+            mm(blk("b5", k, 32), R("bw"), R(X, 32 * k + 31, 4096, 128), True, True)
+        for w in (128, 256, 512):
+            act(R("xrep", w, 2 * w), R("xrep", 0, w), F.Copy)
+        act(R("wb"), R("jtf", 0, 264), F.Copy, None, 0.0)
+        tt(R("mp"), R("b4", 0, 128), MK, A.mult)
+        scan(R("sp"), R("rst"), R("mp"), 0.0, A.mult, A.add)
+        cp(R("ui"), R("sp", 15, 128, 16))
+        ts(R("ub"), R("ui"), 4095, None, A.bitwise_and)
+        tt(R("sq"), R("ub"), R("ub"), A.mult)
+        cp(R("uf"), R("ub"))
+        ts(R("s5"), R("sq"), 5, None, A.arith_shift_right)
+        cp(R("u2"), R("s5"))
+        for k in range(8):
+            ts(R("cv", k, 512, 8), blk("kr", t, 64), R("uf", k, k + 1), R("u2", k, k + 1), A.mult, A.add)
+        for a, b in ((0, 128), (128, 512)):
+            ts(R("ci", a, b), R("cv", a, b), 4095, None, A.bitwise_and)
+            cp(R("cl", a, b), R("ci", a, b))
+        ts(R("c16"), R("cl"), -2048.0, None, A.add)
+
+        def gather_s(k):
+            m0, m1 = SCH[k]
+            act(R("ga", 128 * m0, 128 * m1), R(X), F.Copy, R("cl", 8 * m0, 8 * m1))
+
+        def abs_s(k):
+            for c in range(SCH[k][0] // 4, SCH[k][1] // 4):
+                bank = R("b%d" % (6 + c % 2))
+                mm(bank, R("idb"), blk("ga", c, 512), True, False)
+                mm(bank, R("nid"), R("xrep", 0, 512), False, True)
+            for c in range(SCH[k][0] // 4, SCH[k][1] // 4):
+                act(blk("ab", c, 512), R("b%d" % (6 + c % 2)), F.Abs)
+
+        def dist(m0, m1, stop):
+            if m0 >= LATE:
+                out = R("b7", 8 * (m0 - LATE), 8 * (m1 - LATE))
+            else:
+                out = R("b0", 8 * m0, 8 * m1)
+            for s in range(16):
+                mm(out, blk("ld", s), R("ab", 128 * m0 + s, 128 * m1, 16), False, stop and s == 15)
+
+        e = 8 * LATE
+        gather_s(0)
+        gather_s(1)
+        for k, (m0, m1) in enumerate(VCH):
+            tt(R("d", 128 * m0, 128 * m1), R(X), R("xrep", 0, 128 * (m1 - m0)), A.subtract, R("cl", 8 * m0, 8 * m1))
+            if k < 2:
+                abs_s(k)
+            act(R("ab", 128 * m0, 128 * m1), R("d", 128 * m0, 128 * m1), F.Abs)
+            if k == 1:
+                mm(R("b0"), R("idh"), R("c16"), False, False)
+                dist(SCH[0][0], SCH[0][1], False)
+                dist(VCH[0][0], VCH[0][1], False)
+                dist(SCH[1][0], SCH[1][1], False)
+                mm(R("b7", 0, 512 - e), R("idf"), R("kc", e, 512), True, False)
+                mm(R("b7", 0, 512 - e), R("idh"), R("c16", e, 512), False, False)
+            if 1 <= k and m1 <= LATE:
+                dist(m0, m1, m1 == LATE)
+        dist(LATE, 64, True)
+        if t == 0:
+            for j in range(8):
+                bank, c, w = SEG[j]
+                act(R("ct", CTO[bank] + c, CTO[bank] + c + w), R("ones", 0, w), F.Copy, None, R("tc", j, j + 1))
+        for bank, js in BANKS:
+            mm(R(bank, 0, BANKW[bank]), R("idf"), R("ct", CTO[bank], CTO[bank] + BANKW[bank]), True, False)
+        if t == 0:
+            later_constants()
+        cp(R("hI"), R("b5", 0, 128))
+        ts(R("h63"), R("hI"), 63, None, A.bitwise_and)
+        ts(R("hb"), R("ub"), 63, None, A.bitwise_and)
+        ts(R("h31"), R("hb"), 1.0, 31.0, A.add, A.mult)
+        for bank, a, b in (("b0", 0, e), ("b7", e, 512)):
+            tt(R("gd", a, b), R(bank, 0, b - a), R("th2", a, b), A.is_lt)
+            tt(R("mk", a, b), R(bank, 0, b - a), R("gd", a, b), A.mult)
+        for k in range(8):
+            red(R("bf", k, k + 1), R("mk", k, 512, 8), A.min)
+        ts(R("dio", 0, 8), R("bf"), 2.0 ** -12, 2047.5 + 2.0 ** -13, A.mult, A.add)
+        cp(R("best"), R("bf"))
+        ts(R("jI"), R("best"), 5, 127, A.arith_shift_right, A.bitwise_and)
+        ts(R("oI"), R("best"), 1, 15, A.arith_shift_right, A.bitwise_and)
+        tt(R("jm"), R("jI"), R("il"), A.is_gt)
+        tt(R("dio", 8, 16), R("oI"), R("ioc"), A.add)
+        tt(R("jv"), R("jI"), R("jm"), A.mult)
+        tt(R("ej"), R("jv"), MK, A.mult, E8)
+        tt(R("ed"), R("dio"), R("mk2"), A.mult, R("expl"))
+        seg = {j: R(SEG[j][0], SEG[j][1], SEG[j][1] + SEG[j][2]) for j in range(8)}
+        for bank, js in BANKS:
+            for j in js:
+                mm(seg[j], R("bo27"), R("ej", 0, SEG[j][2]), False, False)
+        for bank, js in BANKS:
+            for j in js:
+                mm(seg[j], R("bo12"), R("ed", 0, SEG[j][2]), False, False)
+                mm(seg[j], R("boh"), R("ed", 128, 128 + SEG[j][2]), False, j == js[-1])
+        ts(blk("b0", 0), R("h63"), 1.0, R("pm"), A.add, A.mult)
+        ts(blk("b0", 1), R("h63"), 1.0, R("pm16"), A.add, A.mult)
+        for bank, js in BANKS:
+            for j in js:
+                red(R("accf", j, j + 1), seg[j], A.min, True)
+        tt(R("acc"), R("accf"), R("self"), A.min)
+        ts(R("fI"), R("acc"), 5, 127, A.arith_shift_right, A.bitwise_and)
+        ts(R("cI"), R("acc"), 31, None, A.bitwise_and)
+        tt(R("ef"), R("fI"), MK, A.mult, E8)
+        mm(R("b5", 0, 128), R("bo"), R("ef"), True, True)
+        cp(R("fl0"), R("fI"))
+        act(R("f0"), R("b5", 0, 128), F.Copy)
+        ts(R("lI"), R("cI"), -1.0, 32.0, A.mult, A.add)
+        tt(R("el"), R("lI"), MK, A.mult, E8)
+        mm(R("b4", 0, 128), R("bo"), R("el"), True, True)
+        mm(R("b6"), R("el"), R("grp", 0, 512), True, True)
+        mm(R("b7"), R("el"), R("grp", 512, 1024), True, True)
+        mm(R("b2"), blk("gsel", 0), R("jt"), True, False)
+        mm(R("b3"), blk("gsel", 0), R("jt"), True, False)
+        gaps = [
+            lambda: red(R("lc"), R("b4", 0, 128), A.add),
+            lambda: (ts(R("kl"), R("kperm"), R("lc"), None, A.mult), ts(R("k31"), R("il"), R("lc"), None, A.mult)),
+            lambda: (ts(R("sk"), R("kl"), 7, None, A.arith_shift_right),
+                     ts(R("s31"), R("k31"), 7, None, A.arith_shift_right)),
+            lambda: (tt(R("pp", 0, 256, 2), R("sk"), blk("b0", 0), A.add),
+                     tt(R("pp", 1, 256, 2), R("sk"), blk("b0", 1), A.add)),
+        ]
+        for k in range(4):
+            fl = R("fl%d" % k)
+            act(R("h%d" % k), R("f%d" % k), F.Copy, fl)
+            gaps[k]()
+            tt(R("mm"), R("h%d" % k), MK, A.mult, fl)
+            act(R("f%d" % (k + 1)), R("h%d" % k), F.Copy, fl)
+            act(blk("lb", k, 256), blk("b%d" % (6 + k // 2), k % 2, 256), F.Copy)
+            scan(R("sc"), R("rst"), R("mm"), 0.0, A.mult, A.add)
+            cp(R("fl%d" % (k + 1)), R("sc", 15, 128, 16))
+        tt(R("b6", 0, 128), R("ac"), R("b4", 0, 128), A.subtract)
+        mm(R("b4", 0, 8), R("idb"), R("kcol"), True, False)
+        act(R("f7"), R("f4"), F.Copy, R("fl4"))
+        ts(R("b6", 256, 512), R("pp"), R("lc"), R("lc"), A.is_ge, A.mult)
+        tt(R("p31"), R("s31"), R("h31"), A.add)
+        tt(R("pw"), R("pp"), R("b6", 256, 512), A.subtract)
+        ts(R("w31"), R("p31"), R("lc"), R("lc"), A.is_ge, A.mult)
+        mm(R("b4", 0, 8), R("f7"), R("gsel", 0, 1024, 128), False, True)
+        act(R("negr", 4, 8), R("b4", 4, 8), F.Copy, None, -1.0)
+        order = (4, 5, 6, 7, 0, 1, 2, 3)
+        for k in order:
+            mm(blk("b2" if k < 4 else "b3", k % 4), blk("gsel", k), R("f7"), False, k % 4 == 3)
+        for k in range(4, 8):
+            mm(R("b5", 0, 128), blk("lb", k), R("omi"), k == 4, False)
+        for k in order:
+            if k < 4:
+                ts(blk("cmp", k), blk("b2", k), R("b4", k, k + 1), None, A.is_gt)
+            else:
+                act(blk("cmp", k), blk("b3", k % 4), F.Sign, None, None, R("negr", k, k + 1))
+        for k in (0, 1, 4, 5, 2, 3, 6, 7):
+            mm(R("b5", 0, 128), blk("lb", k), blk("cmp", k), False, k == 7)
+        tt(R("q31"), R("p31"), R("w31"), A.subtract)
+        cp(R("plist"), R("pw"))
+        cp(R("l31"), R("q31"))
+        tt(R("mp"), R("b5", 0, 128), MK, A.mult)
+        act(R("t4"), R("b5", 0, 128), F.Copy, None, 4095.0)
+        scan(R("sp"), R("rst"), R("mp"), 0.0, A.mult, A.add)
+        ts(R("cell"), R("sp", 15, 128, 16), 0.0625, -0.46875, A.mult, A.add)
+        tt(R("vrow"), R("t4"), R("b6", 0, 128), A.add)
+        cp(R("celll"), R("cell"))
+        cp(R("wb", 8, 264), R("vrow"), None, R("celll"))
+
+        def step(n, a, b):
+            if n == 0:
+                tt(R("b7", a, b), R("wb", 8 + a, 8 + b), R("b1", a, b), A.is_lt)
+            elif n == 1:
+                tt(R("w1", a, b), R("wb", 8 + a, 8 + b), R("b7", a, b), A.mult)
+            elif n == 2:
+                scan(R("ff", a, b), R("wb", 7 + a, 7 + b), R("w1", a, b), R("ff", a - 1, a) if a else 0.0, A.max, A.max)
+            elif n == 3:
+                tt(R("si", a, b), R("ff", a, b), R("b1", 256 + a, 256 + b), A.add)
+            elif n == 4:
+                ts(R("sj", a, b), R("si", a, b), 4095, None, A.bitwise_and)
+            else:
+                cp(R("sl", a, b), R("sj", a, b))
+        for n, second in ((0, 0), (0, 1), (1, 0), (1, 1), (2, 0), (3, 0), (2, 1), (4, 0), (3, 1), (5, 0), (4, 1), (5, 1)):
+            if second:
+                step(n, LAYS, 256)
+            else:
+                step(n, 0, LAYS)
+        act(R("lay", 0, 16 * LAYS), R(X), F.Copy, R("sl", 0, LAYS))
+        cp(R("lay", 16 * LAYS, 4096), R(X), R("sl", LAYS, 256))
+        to = blk(Xn, rank, MB)
+
+        def kids(q, kr, a, b):
+            buf, o = (ko, MB * (kr - 1)) if kr else (Xn, MB * rank)
+            lst = R("plist", 64 * kr + a, 64 * kr + b)
+            if q == "V":
+                cp(R(buf, o + 16 * a, o + 16 * b), R("lay"), lst)
+            else:
+                act(R(buf, o + 16 * a, o + 16 * b), R("lay"), F.Copy, lst)
+
+        def send(krs, buf, into, rs, ls):
+            dsts = [T.cores[(kr + rank) % N] for kr in krs]
+            ids = [DstId(rid=topo.addr(dst)[0], pnc=topo.addr(dst)[1]) for dst in dsts]
+            sync("G", [], [buf])
+            g.remote_dma_fused([RemoteDMATransfer(dst_ids=ids, dma_engine_mask=topo.mask(core, dsts[0]), srcs=[ap(buf)],
+                                                  dsts=[ap(into) for _ in krs], remote_sem=T.sem[rs])],
+                               local_sem=T.sem[ls])
+        if t < 2:
+            lr = "lr%d" % t
+            cp(blk(lr, rank), R("lay"), R("l31"))
+            send((1, 2, 3), blk(lr, rank), blk(lr, rank), "sm%d" % t, "lq%d" % t)
+            arrive("sm%d" % t, 3 * ne, [blk(lr, r) for r in range(N) if r != rank])
+            extra.append(("lq%d" % t, ne))
+        for kr in far + near + [0]:
+            kids("V", kr, 0, 32)
+            kids("S", kr, 32, 64)
+            if kr:
+                send((kr,), blk(ko, kr - 1, MB), to, "ar%d_%d" % (t, kr), "ls%d" % t)
+        extra.append(("ls%d" % t, 3 * ne))
+        for kr in (1, 2, 3):
+            arrive("ar%d_%d" % (t, kr), ne, [blk(Xn, (rank - kr) % N, MB)])
+    for kr in [0] + [(-k) % N for k in far + near]:
+        s = (rank - kr) % N
+        dma("Y", T.y[:, MB * s:MB * s + MB], T.x3[:, MB * s:MB * s + MB], [], [blk("x3", s, MB)])
+    finish(extra)

@@ -14,24 +14,30 @@ for _bank, _js in BANKS:
         _c += 16 * (_j + 1)
 BANKW = {"b2": 240, "b3": 176, "b4": 160}
 CTO = {"b2": 0, "b3": 240, "b4": 416}
-SCH = [(0, 8), (8, 16)]
-VCH = [(16, 24), (24, 32), (32, 40), (40, 48), (48, 56), (56, 60), (60, 64)]
 LATE = 56
+_plan = """c16 0 0; gs 0 8; gs 8 16; gv 16 24; gv 24 32; sub 0 4; sub 4 8; d 16 24; abs 0 4; abs 4 8; neg 16 24; sub 8 12;
+sub 12 16; gv 32 40; abs 8 12; abs 12 16; ab 0 8; ab 16 24; as 24 32; ab 8 16; h 0 0; gv 40 48; as 32 40; ab 24 32;
+gv 48 56; as 40 48; ab 32 40; gv 56 64; as 48 56; ab 40 48; ab 48 56; end 0 56; neg 56 64; d 56 64; good 0 56; ab 56 64;
+end 56 64; good 56 64"""
+PLAN = [(w.split()[0], int(w.split()[1]), int(w.split()[2])) for w in _plan.split(";")]
 LAYS = 136
+DIFF = (("b2", 0, "V"), ("b3", 4, "S"), ("b6", 2, "V"), ("b7", 6, "S"))
+M23, M28, M29 = 1.5 * 2.0 ** 23, 1.5 * 2.0 ** 28, 1.5 * 2.0 ** 29
 
 _f, _h, _b, _i, _u = "float32", "float16", "bfloat16", "int32", "uint16"
 _sb = {
-    _b: "x0:4096 x1:4096 x2:4096 x3:4096 lay:4096 ko0:3072 ko1:3072 ko2:3072 lr0:512 lr1:512 q16:128 q17:128 bq:128 "
-        "bo:128 bo27:128 mk2:256 idb:128 nid:128 ld:2048 bw:128 ones:128 omi:128 gsel:1024 grp:1024 jt:512 kcol:8 "
-        "rst:128 xrep:1024 ga:2048 d:8192 ab:8192 gd:512 ej:128 ef:128 el:128 mm:128 lb:1024 cmp:1024 "
-        "f0:128 f1:128 f2:128 f3:128 f4:128 f7:128 h0:128 h1:128 h2:128 h3:128",
+    _b: "x0:4096 x1:4096 x2:4096 x3:4096 lay:4096 ko0:3072 ko1:3072 ko2:3072 xr0:1024 xr1:1024 xr2:1024 lo0:128 lo1:128 "
+        "q16:128 bo:128 bo27:128 mk2:256 idb:128 nid:128 ldw:144 bww:144 bw:128 ones:512 omi:128 grp:256 "
+        "ca:128 cr:576 b26:128 kcl:128 dl:128 dr:256 hc:128 pc:128 ac:128 nbo:128 "
+        "rst:128 d:8192 ab:8192 gd:512 ej:128 ef:128 el:128 mm:128 lb:256 cmp:1024 "
+        "f0:128 f1:128 f2:128 f3:128 f4:128 f5:128 f6:128 h0:128 h1:128 h2:128 h3:128 lf:128 rt:128",
     _h: "bo12:128 boh:128 idh:128 c16:512 ed:256",
-    _f: "wtf:1 ekt:256 kr:192 th2:512 pf:1 pm:1 pm16:1 pm4:1 pg:1 row:128 mg:128 bof:128 idf:128 i16:8 i1:8 gc:8 "
-        "pgc:8 negr:8 jtf:512 kc:512 il:8 eq0:8 tgt:8 tc:8 ct:576 self:8 ioc:8 pl:256 kperm:128 ac:128 uf:8 u2:8 "
-        "h31:8 w31:8 q31:8 mk:512 bf:8 jm:8 accf:8 sc:128 lc:1 pp:256 pw:256 mp:128 t4:128 vrow:128 sp:128 wb:264 "
+    _f: "wtf:1 ekt:256 kr:192 th2:512 pf:1 pm:1 pm16:1 pm4:1 pg:1 pe:1 po:1 pw2:1 gk:1 gs:1 sl_:1 bl:1 sr:1 br:1 qb:1 qb16:1 "
+        "row:144 mg:128 gi:256 bof:128 sel:144 s15:1 mks:128 i16:8 il:8 self:8 ioc:8 pl:256 kperm:128 pw3:1 tc:8 uf:8 u2:8 sq:8 "
+        "mk:512 bf:8 accf:8 sc:128 lc:1 pp:256 pw:256 mp:128 t4:128 vrow:128 sp:128 wb:264 hr:128 hf:128 "
         "w1:256 ff:256",
-    _i: "wti:1 kt:16 pi:1 pmi:1 pgi:1 expi:16 ui:8 ub:8 sq:8 s5:8 cv:512 ci:512 best:8 jI:8 oI:8 jv:8 dio:16 "
-        "acc:8 fI:8 cI:8 lI:8 hI:128 h63:128 kl:128 sk:128 hb:8 k31:8 s31:8 p31:8 cell:8 si:256 sj:256",
+    _i: "wti:1 kt:16 pi:1 pmi:1 pgi:1 poi:1 expi:16 ui:8 ub:8 cv:512 ci:512 best:8 jI:8 oI:8 dio:16 "
+        "acc:8 fI:8 cI:8 lI:8 sk:128 si:256 sj:256",
     _u: "expl:16 cl:512 plist:256 celll:8 l31:8 sl:256 fl0:8 fl1:8 fl2:8 fl3:8 fl4:8",
 }
 WIDTH, TYPE, PLACE, SCRATCH, _used = {}, {}, {}, {}, {}
@@ -60,6 +66,7 @@ def build_tracker(g, T):
     snap = {}
     acc = {}
     ndma = [0]
+    base = [0]
 
     def meet(r, e):
         if r[1] >= e[3] or e[2] >= r[2]:
@@ -99,6 +106,11 @@ def build_tracker(g, T):
 
     def emit(q, call, outs, ins):
         sync(q, outs, ins)
+        if q == "G":
+            if outs[0][4] != base[0] and clk[q].get("qG", 0) < cnt[q]:
+                g.wait_ge(T.sem["qG"], cnt[q])
+                clk[q]["qG"] = cnt[q]
+            base[0] = outs[0][4]
         cnt[q] += 1
         call(eng[q]).then_inc(T.sem["q" + q], 1)
         done(q, q, ("q" + q, cnt[q]), outs, ins)
@@ -113,6 +125,10 @@ def build_tracker(g, T):
     def arrive(s, val, outs):
         done(None, s, (s, val), outs, ())
 
+    def fence():
+        n = cnt["P"]
+        return lambda: g.tensor.wait_ge(T.sem["qP"], n)
+
     def finish(extra):
         for q in ("V", "S", "P", "G"):
             g.wait_ge(T.sem["q" + q], cnt[q])
@@ -120,26 +136,27 @@ def build_tracker(g, T):
             g.wait_ge(T.sem["dl%d" % k], 16)
         for s, v in extra:
             g.wait_ge(T.sem[s], v)
-    return emit, dma, sync, arrive, finish
+    return emit, dma, sync, arrive, fence, finish
 
 
 def rank_program(g, core, T, topo):
     rank = T.rank_of(core)
     if rank is None:
         return
-    emit, dma, sync, arrive, finish = build_tracker(g, T)
+    emit, dma, sync, arrive, fence, finish = build_tracker(g, T)
 
     def R(name, a=0, b=None, st=1):
         p, o = PLACE[name]
-        return (p, o + a, o + (WIDTH[name] if b is None else b), st)
+        return (p, o + a, o + (WIDTH[name] if b is None else b), st, 0, 128)
 
     def blk(name, k, w=128):
         return R(name, w * k, w * k + w)
 
+    def rows(r, p0, p1):
+        return r[:4] + (p0, p1)
+
     def ap(r):
-        if r[3] == 1:
-            return T[r[0]][:, r[1]:r[2]]
-        return T[r[0]][:, r[1]:r[2]:r[3]]
+        return T[r[0]][r[4]:r[5], r[1]:r[2]:r[3]] if r[3] > 1 else T[r[0]][r[4]:r[5], r[1]:r[2]]
 
     def src(r, idx):
         return ap(r) if idx is None else ap(r).indirect(ap(idx))
@@ -153,11 +170,12 @@ def rank_program(g, core, T, topo):
     def tt(out, in0, in1, op, idx=None):
         emit("V", lambda e: e.tensor_tensor(ap(out), src(in0, idx), ap(in1), op), [out], regs(in0, in1, idx))
 
-    def ts(out, in0, s1, s2, op0, op1=None):
+    def ts(out, in0, s1, s2, op0, op1=None, idx=None):
         if op1 is None:
             emit("V", lambda e: e.tensor_scalar(ap(out), ap(in0), sca(s1), None, op0), [out], regs(in0, s1))
         else:
-            emit("V", lambda e: e.tensor_scalar(ap(out), ap(in0), sca(s1), sca(s2), op0, op1), [out], regs(in0, s1, s2))
+            emit("V", lambda e: e.tensor_scalar(ap(out), src(in0, idx), sca(s1), sca(s2), op0, op1), [out],
+                 regs(in0, s1, s2, idx))
 
     def cp(out, in_, idx=None, oidx=None):
         emit("V", lambda e: e.tensor_copy(src(out, oidx), src(in_, idx)), [out], regs(in_, idx, oidx))
@@ -182,82 +200,118 @@ def rank_program(g, core, T, topo):
     def mm(out, lhsT, rhs, start, stop):
         emit("P", lambda e: e.matmul(ap(out), ap(lhsT), ap(rhs), start, stop), [out], [lhsT, rhs])
 
-    def iota(name, pattern, cm=0):
-        out = R(name)
-        kw = {} if TYPE[name] == _i else {"allow_small_or_imprecise_dtypes": True}
-        emit("G", lambda e: e.iota(ap(out), pattern, 0, cm, **kw), [out], [])
+    def iota(out, pattern, cm=0, base=0):
+        kw = {} if out[0].endswith(_i) else {"allow_small_or_imprecise_dtypes": True}
+        emit("G", lambda e: e.iota(ap(out), pattern, base, cm, **kw), [out], [])
 
-    dma("Y", T.x0[:], T.gen0[:], [R("x0")], [])
-    dma("S", T.kt[:, 0:12], T.km[:], [R("kt", 0, 12)], [])
-    dma("S", T.kt[:, 12:16], T.th[:], [R("kt", 12, 16)], [])
+    def select(out, in_, pattern, op, other, base, cm):
+        emit("G", lambda e: e.affine_select(ap(out), ap(in_), pattern, op, other, base, cm), [out], [in_])
+
+    def setrow(r, p, v):
+        select(r, r, [[0, r[2] - r[1]]], A.not_equal, v, r[4] - p, 1)
+
+    def band(name, s):
+        return R(name, 15 - s, 143 - s)
+
     dma("S", T.wti[:], T.wt[:], [R("wti")], [])
+    dma("Y", T.kt[:, 0:12], T.km[:], [R("kt", 0, 12)], [])
+    dma("Y", T.kt[:, 12:16], T.th[:], [R("kt", 12, 16)], [])
+    dma("Y", T.x0[:], T.gen0[:], [R("x0")], [])
 
-    iota("pi", [[0, 1]], 1)
-    iota("q16", [[0, 8], [1, 16]])
-    iota("mg", [[1, 8], [0, 16]])
-    iota("expi", [[1, 16]])
-    iota("row", [[1, 128]])
-    iota("i16", [[16, 8]])
-    iota("i1", [[1, 8]])
-    iota("kperm", [[1, 4], [4, 32]])
-    iota("jtf", [[0, 4], [1, 128]])
-    iota("pl", [[16, 256]])
+    iota(R("pi"), [[0, 1]], 1)
+    iota(R("row"), [[1, 144]])
+    iota(R("q16"), [[0, 8], [1, 16]])
+    iota(R("mg"), [[1, 8], [0, 16]])
+    iota(R("expi"), [[1, 16]])
+    iota(R("i16"), [[16, 8]])
+    iota(R("pl"), [[16, 256]])
+    iota(R("kperm"), [[1, 4], [4, 32]])
+    iota(R("gi"), [[1, 8], [8, 2], [0, 16]])
     MK = R("mk2", 0, 128)
     E8 = R("expl", 0, 8)
-    cp(R("pf"), R("pi"))
+    ROW = R("row", 0, 128)
+    ONE = R("ones", 0, 128)
+
+    def top(r):
+        return rows(r, 0, 32)
+
+    def lin(out, in_, scale, bias=0.0):
+        act(out, in_, F.Identity, None, scale, bias)
     ts(R("pmi"), R("pi"), 15, None, A.bitwise_and)
     ts(R("pgi"), R("pi"), 4, None, A.arith_shift_right)
-    cp(R("expl"), R("expi"))
+    cp(R("pf"), R("pi"))
     cp(R("pm"), R("pmi"))
     cp(R("pg"), R("pgi"))
-    ts(R("q17"), R("q16"), 1.0, None, A.add)
-    ts(R("bo"), R("mg"), R("pg"), None, A.is_equal)
-    ts(R("bof"), R("mg"), R("pg"), None, A.is_equal)
+    ts(R("poi"), R("pgi"), 1, None, A.bitwise_and)
+    fill(R("ones"), 1.0)
+    ts(R("pe"), R("pg"), 16.0, 15.0, A.mult, A.add)
+    cp(R("po"), R("poi"))
+    ts(R("sl_"), R("pm"), 1.0, None, A.is_equal)
+    ts(R("sr"), R("pm"), 0.0, None, A.is_equal)
+    ts(R("s15"), R("pm"), 15.0, None, A.is_equal)
+    ts(R("gs"), R("pg"), 3.5, -0.5, A.is_gt, A.mult)
+    ts(R("ldw"), R("row"), R("pe"), 4096.0, A.is_equal, A.mult)
+    ts(R("idb"), ROW, R("pf"), None, A.is_equal)
     ts(MK, R("q16"), R("pm"), None, A.is_equal)
     ts(R("mk2", 128, 256), R("q16"), R("pm"), None, A.is_equal)
-    tt(R("bq"), R("q17"), R("bo"), A.mult)
-    for s in range(16):
-        ts(blk("ld", s), R("bq"), float(s + 1), 4096.0, A.is_equal, A.mult)
-    cp(R("wtf"), R("wti"))
-    ts(R("bw"), R("bo"), R("wtf"), None, A.mult)
-    tt(R("ekt"), R("kt"), R("mk2"), A.mult, R("expl"))
-    mm(R("b1", 0, 256), R("bof"), R("ekt"), True, True)
-    ts(R("idf"), R("row"), R("pf"), None, A.is_equal)
-    ts(R("idb"), R("row"), R("pf"), None, A.is_equal)
-    ts(R("nid"), R("row"), R("pf"), -1.0, A.is_equal, A.mult)
-    ts(R("idh"), R("row"), R("pf"), None, A.is_equal)
     ts(R("rst"), R("q16"), 0.0, None, A.is_gt)
-    fill(R("ones"), 1.0)
-    ts(R("il"), R("i16"), R("pm"), None, A.add)
-    ts(R("pgc"), R("i1"), R("pg"), None, A.is_equal)
-    ts(R("gc"), R("i16"), R("pf"), 128.0, A.is_equal, A.mult)
-    ts(R("eq0"), R("il"), 0.0, None, A.is_equal)
-    ts(R("pm16"), R("pm"), 16.0, None, A.add)
-    ts(R("pm4"), R("pm"), 4095.0, 4095.0, A.mult, A.add)
-    tt(R("tgt"), R("il"), R("eq0"), A.subtract)
-    ts(R("pgc", 4, 8), R("pgc", 4, 8), 0.5, None, A.mult)
-    ts(R("self"), R("il"), 32.0, 4095.0 * 4096.0, A.mult, A.add)
-    ts(R("tc"), R("tgt"), -(2.0 ** 27), 2.0 ** 23 + 2048.0, A.mult, A.add)
-    ts(R("ioc"), R("il"), 32.0, 1.0 - 2048.0, A.mult, A.add)
-    ts(R("kcol"), R("ones", 0, 8), R("pf"), None, A.mult)
-    ts(R("omi"), R("row"), R("pf"), None, A.not_equal)
-    act(R("bo27"), R("bo"), F.Copy, None, 2.0 ** 27)
-    act(R("bo12"), R("bo"), F.Copy, None, 4096.0)
-    act(R("boh"), R("bo"), F.Copy)
-    act(R("kc"), R("jtf"), F.Identity, None, 0.0, 2048.0 - 2.0 ** 24)
-    act(R("kr"), R("b1", 0, 192), F.Copy)
+    ts(top(R("ca")), top(R("q16")), top(R("pf")), None, A.is_equal)
+    ts(R("bof"), R("mg"), R("pg"), None, A.is_equal)
+    cp(R("expl"), R("expi"))
+    for name, v in (("kcl", 2048.0), ("b26", 2.0 ** 26), ("hc", -31.5), ("pc", -7.0)):
+        lin(top(R(name)), top(ROW), 0.0, v)
+    lin(R("pm16"), R("pm"), 1.0, 16.0)
+    lin(R("pm4"), R("pm"), 4095.0, 4095.0)
+    lin(R("qb"), R("pm"), 32.5)
+    lin(R("qb16"), R("pm"), 32.5, 16 * 32.5)
+    lin(R("pw2"), R("po"), 128.0 * 16383.0, 128.0)
+    lin(R("pw3"), R("po"), -128.0 * 16383.0, -128.0)
+    lin(R("gk"), R("po"), 8.0, R("pg"))
+    lin(R("gs"), R("gs"), 1.0, 1.0)
+    lin(R("bl"), R("sr"), R("pw2"))
+    lin(R("br"), R("sl_"), R("pw3"))
+    lin(R("il"), R("i16"), 1.0, R("pm"))
+    lin(R("self"), R("il"), 32.0, 4095.0 * 4096.0)
+    lin(R("ioc"), R("il"), 32.0, 1.0 - 2048.0)
+    cp(R("wtf"), R("wti"))
+    tt(R("ekt"), R("kt"), R("mk2"), A.mult, R("expl"))
+    ts(R("bww"), R("row"), R("pe"), R("wtf"), A.is_equal, A.mult)
+    mm(R("b7", 0, 256), R("bof"), R("ekt"), True, True)
+    lin(R("nid"), R("idb"), -1.0)
+    lin(R("kr"), R("b7", 0, 192), 32.0)
     for k in range(8):
-        act(R("th2", k, 512, 8), R("b1", 192, 256), F.Identity, None, 4096.0, -(2.0 ** 24))
-    act(R("b1", 256, 512), R("pl"), F.Identity, None, None, R("pm"))
-    act(R("b1", 0, 256), R("pl"), F.Identity, None, 4095.0, R("pm4"))
+        lin(R("th2", k, 512, 8), R("b7", 192, 256), 4096.0, -(2.0 ** 24))
+    ts(R("sel"), R("row"), R("pe"), R("s15"), A.is_equal, A.mult)
+    ts(R("grp"), R("gi"), R("gk"), R("gs"), A.is_equal, A.mult)
+    ts(R("b1", 256, 512), R("pl"), R("pm"), None, A.add)
+    ts(R("b1", 0, 256), R("pl"), 4095.0, R("pm4"), A.mult, A.add)
+    for name, scale in (("bw", R("wtf")), ("bo", 1.0), ("nbo", -1.0), ("bo27", 2.0 ** 27), ("bo12", 4096.0), ("boh", 1.0)):
+        ts(R(name), R("mg"), R("pg"), scale, A.is_equal, A.mult)
+    lin(R("idh"), R("idb"), 1.0)
+    lin(R("kperm"), R("kperm"), 1.0 / 128.0)
+    lin(R("omi"), R("idb"), -1.0, 1.0)
+    lin(R("mks"), MK, (1.0 - 2.0 ** -13) / 16.0)
+    setrow(top(R("kcl")), 0, -(2.0 ** 24))
+    mid = rows(R("tc"), 32, 64)
+    iota(mid, [[16, 8]])
+    for p, v in ((32, 1.0), (34, -(2.0 ** -4)), (35, -(2.0 ** -16))):
+        setrow(mid, p, v)
+    lin(mid, mid, -(2.0 ** 27))
+    select(rows(R("ca"), 32, 64), rows(R("q16"), 32, 64), [[0, 128]], A.is_equal, 1.0, 0, 1)
+    for j in range(8):
+        bank, c, w = SEG[j]
+        piece = R("cr", CTO[bank] + c, CTO[bank] + c + w)
+        lin(rows(piece, 32, 64), rows(R("ones", 0, w), 32, 64), rows(R("tc", j, j + 1), 32, 64))
+        select(top(piece), top(R("b26", 0, w)), [[1, w]], A.is_ge, 0.0, -16 * j, -1)
+    iota(top(R("dl")), [[1, 128]])
+    setrow(top(R("dl")), 0, 1.0)
+    for k, w in enumerate((1, 16384)):
+        iota(top(blk("dr", k)), [[w, 128]])
+        setrow(top(blk("dr", k)), 1, -float(w))
+    iota(top(R("ac")), [[32, 128]])
+    setrow(top(R("ac")), 1, 28672.0)
+    setrow(top(R("ac")), 2, 25.0)
 
-    def later_constants():
-        for k in range(8):
-            act(blk("grp", k), R("bo"), F.Copy, None, R("pgc", k, k + 1))
-        act(R("jt"), R("jtf"), F.Copy, None, 1.0 / 128.0)
-        act(R("ac"), R("row"), F.Identity, None, 32.0, 32.0)
-        for k in range(8):
-            act(blk("gsel", k), R("ones"), F.Copy, None, R("gc", k, k + 1))
     extra = []
     ne = len(topo.engines(core, T.cores[(rank + 1) % N]))
     far = [kr for kr in (1, 2, 3) if topo.die(T.cores[(kr + rank) % N]) != topo.die(core)]
@@ -267,98 +321,84 @@ def rank_program(g, core, T, topo):
         X = "x%d" % t
         Xn = "x%d" % (t + 1)
         ko = "ko%d" % t
-        for r in range(N):
-            if t:
-                last = R("lr%d" % (t - 1), 128 * r + (rank - r) % N, 128 * r + 128, 4)
-            else:
-                last = R(X, MB * r + 31, MB * r + MB, 32)
-            mm(blk("b4", r, 32), R("bw"), last, True, True)
-            act(blk("xrep", r, 32), last, F.Copy)
-        mm(R("b0"), R("idf"), R("kc"), True, False)
-        for k in range(4):
-            mm(blk("b5", k, 32), R("bw"), R(X, 32 * k + 31, 4096, 128), True, True)
+        xr = "xr%d" % t
+
+        def last(a, st):
+            return R(xr, a, 128, st) if t else R(X, 32 * a + 31, 4096, 32 * st)
+        for s in range(16):
+            mm(R("b4", 0, 8), band("bww", s), last(s, 16), s == 0, s == 15)
+        if t == 0:
+            act(R(xr, 0, 128), last(0, 1), F.Copy)
         for w in (128, 256, 512):
-            act(R("xrep", w, 2 * w), R("xrep", 0, w), F.Copy)
-        act(R("wb"), R("jtf", 0, 264), F.Copy, None, 0.0)
-        tt(R("mp"), R("b4", 0, 128), MK, A.mult)
-        scan(R("sp"), R("rst"), R("mp"), 0.0, A.mult, A.add)
-        cp(R("ui"), R("sp", 15, 128, 16))
+            act(R(xr, w, 2 * w), R(xr, 0, w), F.Copy)
+        e = 8 * LATE
+        mm(R("b0", 0, e), rows(R("kcl"), 0, 2), rows(R("ones", 0, e), 0, 2), True, False)
+        mm(R("b5", 0, 512 - e), rows(R("kcl"), 0, 2), rows(R("ones", 0, 512 - e), 0, 2), True, False)
+        iota(R("wb"), [[0, 264]])
+        cp(R("ui"), R("b4", 0, 8))
         ts(R("ub"), R("ui"), 4095, None, A.bitwise_and)
         tt(R("sq"), R("ub"), R("ub"), A.mult)
-        cp(R("uf"), R("ub"))
-        ts(R("s5"), R("sq"), 5, None, A.arith_shift_right)
-        cp(R("u2"), R("s5"))
+        ts(R("uf"), R("ub"), -4096.0, None, A.add)
+        ts(R("u2"), R("sq"), -15.0, M28, A.add, A.add)
         for k in range(8):
             ts(R("cv", k, 512, 8), blk("kr", t, 64), R("uf", k, k + 1), R("u2", k, k + 1), A.mult, A.add)
-        for a, b in ((0, 128), (128, 512)):
-            ts(R("ci", a, b), R("cv", a, b), 4095, None, A.bitwise_and)
+        for a, b in ((0, 64), (64, 512)):
+            ts(R("ci", a, b), R("cv", a, b), 5, 4095, A.arith_shift_right, A.bitwise_and)
             cp(R("cl", a, b), R("ci", a, b))
-        ts(R("c16"), R("cl"), -2048.0, None, A.add)
 
-        def gather_s(k):
-            m0, m1 = SCH[k]
-            act(R("ga", 128 * m0, 128 * m1), R(X), F.Copy, R("cl", 8 * m0, 8 * m1))
+        def wide(name, m0, m1):
+            return R(name, 128 * m0, 128 * m1)
 
-        def abs_s(k):
-            for c in range(SCH[k][0] // 4, SCH[k][1] // 4):
-                bank = R("b%d" % (6 + c % 2))
-                mm(bank, R("idb"), blk("ga", c, 512), True, False)
-                mm(bank, R("nid"), R("xrep", 0, 512), False, True)
-            for c in range(SCH[k][0] // 4, SCH[k][1] // 4):
-                act(blk("ab", c, 512), R("b%d" % (6 + c % 2)), F.Abs)
-
-        def dist(m0, m1, stop):
-            if m0 >= LATE:
-                out = R("b7", 8 * (m0 - LATE), 8 * (m1 - LATE))
-            else:
-                out = R("b0", 8 * m0, 8 * m1)
-            for s in range(16):
-                mm(out, blk("ld", s), R("ab", 128 * m0 + s, 128 * m1, 16), False, stop and s == 15)
-
-        e = 8 * LATE
-        gather_s(0)
-        gather_s(1)
-        for k, (m0, m1) in enumerate(VCH):
-            tt(R("d", 128 * m0, 128 * m1), R(X), R("xrep", 0, 128 * (m1 - m0)), A.subtract, R("cl", 8 * m0, 8 * m1))
-            if k < 2:
-                abs_s(k)
-            act(R("ab", 128 * m0, 128 * m1), R("d", 128 * m0, 128 * m1), F.Abs)
-            if k == 1:
-                mm(R("b0"), R("idh"), R("c16"), False, False)
-                dist(SCH[0][0], SCH[0][1], False)
-                dist(VCH[0][0], VCH[0][1], False)
-                dist(SCH[1][0], SCH[1][1], False)
-                mm(R("b7", 0, 512 - e), R("idf"), R("kc", e, 512), True, False)
-                mm(R("b7", 0, 512 - e), R("idh"), R("c16", e, 512), False, False)
-            if 1 <= k and m1 <= LATE:
-                dist(m0, m1, m1 == LATE)
-        dist(LATE, 64, True)
-        if t == 0:
-            for j in range(8):
-                bank, c, w = SEG[j]
-                act(R("ct", CTO[bank] + c, CTO[bank] + c + w), R("ones", 0, w), F.Copy, None, R("tc", j, j + 1))
-        for bank, js in BANKS:
-            mm(R(bank, 0, BANKW[bank]), R("idf"), R("ct", CTO[bank], CTO[bank] + BANKW[bank]), True, False)
-        if t == 0:
-            later_constants()
-        cp(R("hI"), R("b5", 0, 128))
-        ts(R("h63"), R("hI"), 63, None, A.bitwise_and)
-        ts(R("hb"), R("ub"), 63, None, A.bitwise_and)
-        ts(R("h31"), R("hb"), 1.0, 31.0, A.add, A.mult)
-        for bank, a, b in (("b0", 0, e), ("b7", e, 512)):
+        def good(bank, a, b):
             tt(R("gd", a, b), R(bank, 0, b - a), R("th2", a, b), A.is_lt)
             tt(R("mk", a, b), R(bank, 0, b - a), R("gd", a, b), A.mult)
+
+        for what, m0, m1 in PLAN:
+            d, ab, lst = wide("d", m0, m1), wide("ab", m0, m1), R("cl", 8 * m0, 8 * m1)
+            bank = R("b%d" % (6 + m0 // 4 % 2), 0, 128 * (m1 - m0))
+            if what == "gs":
+                act(d, R(X), F.Copy, lst)
+            elif what == "sub":
+                mm(bank, R("idb"), d, True, False)
+                mm(bank, R("nid"), R(xr, 0, 128 * (m1 - m0)), False, True)
+            elif what == "abs":
+                act(ab, bank, F.Abs)
+            elif what == "gv":
+                tt(d, R(X), R(xr, 0, 128 * (m1 - m0)), A.subtract, lst)
+            elif what == "as":
+                act(ab, d, F.Abs)
+            elif what == "neg":
+                ts(ab, d, 0.0, -2.0, A.min, A.mult)
+            elif what in ("d", "ab"):
+                out = R("b5", 8 * (m0 - LATE), 8 * (m1 - LATE)) if m0 >= LATE else R("b0", 8 * m0, 8 * m1)
+                for s in range(16):
+                    mm(out, band("ldw", s), R(what, 128 * m0 + s, 128 * m1, 16), False, False)
+            elif what == "c16":
+                ts(R("c16"), R("cl"), -2048.0, None, A.add)
+            elif what == "end":
+                mm(R("b5" if m0 else "b0", 0, 8 * (m1 - m0)), R("idh"), R("c16", 8 * m0, 8 * m1), False, True)
+            elif what == "good":
+                good("b5" if m0 else "b0", 8 * m0, 8 * m1)
+            else:
+                mm(R("b6", 0, 128), rows(R("hc"), 0, 1), rows(ONE, 0, 1), True, False)
+                for k in range(4):
+                    mm(blk("b6", k, 32), R("bw"), last(k, 4), False, k == 3)
+        for bank, js in BANKS:
+            mm(R(bank, 0, BANKW[bank]), rows(R("ca"), 0, 36), rows(R("cr", CTO[bank], CTO[bank] + BANKW[bank]), 0, 36),
+               True, False)
         for k in range(8):
             red(R("bf", k, k + 1), R("mk", k, 512, 8), A.min)
-        ts(R("dio", 0, 8), R("bf"), 2.0 ** -12, 2047.5 + 2.0 ** -13, A.mult, A.add)
         cp(R("best"), R("bf"))
+        ts(R("dio", 0, 8), R("bf"), 2.0 ** -12, 2047.5 + 2.0 ** -13, A.mult, A.add)
         ts(R("jI"), R("best"), 5, 127, A.arith_shift_right, A.bitwise_and)
         ts(R("oI"), R("best"), 1, 15, A.arith_shift_right, A.bitwise_and)
-        tt(R("jm"), R("jI"), R("il"), A.is_gt)
+        tt(R("ej"), R("jI"), MK, A.mult, E8)
         tt(R("dio", 8, 16), R("oI"), R("ioc"), A.add)
-        tt(R("jv"), R("jI"), R("jm"), A.mult)
-        tt(R("ej"), R("jv"), MK, A.mult, E8)
         tt(R("ed"), R("dio"), R("mk2"), A.mult, R("expl"))
+        ts(R("hr"), R("b6", 0, 128), M29, -M29, A.add, A.add)
+        tt(R("hf"), R("b6", 0, 128), R("hr"), A.subtract)
+        lin(blk("b0", 0), R("hf"), R("pm"), R("qb"))
+        lin(blk("b0", 1), R("hf"), R("pm16"), R("qb16"))
         seg = {j: R(SEG[j][0], SEG[j][1], SEG[j][1] + SEG[j][2]) for j in range(8)}
         for bank, js in BANKS:
             for j in js:
@@ -367,8 +407,6 @@ def rank_program(g, core, T, topo):
             for j in js:
                 mm(seg[j], R("bo12"), R("ed", 0, SEG[j][2]), False, False)
                 mm(seg[j], R("boh"), R("ed", 128, 128 + SEG[j][2]), False, j == js[-1])
-        ts(blk("b0", 0), R("h63"), 1.0, R("pm"), A.add, A.mult)
-        ts(blk("b0", 1), R("h63"), 1.0, R("pm16"), A.add, A.mult)
         for bank, js in BANKS:
             for j in js:
                 red(R("accf", j, j + 1), seg[j], A.min, True)
@@ -382,57 +420,63 @@ def rank_program(g, core, T, topo):
         ts(R("lI"), R("cI"), -1.0, 32.0, A.mult, A.add)
         tt(R("el"), R("lI"), MK, A.mult, E8)
         mm(R("b4", 0, 128), R("bo"), R("el"), True, True)
-        mm(R("b6"), R("el"), R("grp", 0, 512), True, True)
-        mm(R("b7"), R("el"), R("grp", 512, 1024), True, True)
-        mm(R("b2"), blk("gsel", 0), R("jt"), True, False)
-        mm(R("b3"), blk("gsel", 0), R("jt"), True, False)
+        mm(R("b5", 128, 384), R("el"), R("grp"), True, True)
+        mm(R("b3", 256, 384), rows(ONE, 0, 3), rows(R("ac"), 0, 3), True, False)
+        mm(R("b3", 256, 384), R("nbo"), R("el"), False, True)
+        for bank, g0, q in DIFF:
+            mm(R(bank, 0, 256), rows(R("dl"), 0, 2), rows(R("dr"), 0, 2), True, False)
+        begun = fence()
         gaps = [
             lambda: red(R("lc"), R("b4", 0, 128), A.add),
-            lambda: (ts(R("kl"), R("kperm"), R("lc"), None, A.mult), ts(R("k31"), R("il"), R("lc"), None, A.mult)),
-            lambda: (ts(R("sk"), R("kl"), 7, None, A.arith_shift_right),
-                     ts(R("s31"), R("k31"), 7, None, A.arith_shift_right)),
-            lambda: (tt(R("pp", 0, 256, 2), R("sk"), blk("b0", 0), A.add),
-                     tt(R("pp", 1, 256, 2), R("sk"), blk("b0", 1), A.add)),
+            lambda: ts(R("sk"), R("kperm"), R("lc"), -63.5 / 128.0, A.mult, A.add),
+            lambda: None,
+            lambda: None,
         ]
         for k in range(4):
             fl = R("fl%d" % k)
+            tt(R("mm"), R("f%d" % k), MK, A.mult, fl)
             act(R("h%d" % k), R("f%d" % k), F.Copy, fl)
-            gaps[k]()
-            tt(R("mm"), R("h%d" % k), MK, A.mult, fl)
             act(R("f%d" % (k + 1)), R("h%d" % k), F.Copy, fl)
-            act(blk("lb", k, 256), blk("b%d" % (6 + k // 2), k % 2, 256), F.Copy)
+            if k == 0:
+                act(R("lb"), R("b5", 128, 384), F.Copy)
             scan(R("sc"), R("rst"), R("mm"), 0.0, A.mult, A.add)
+            gaps[k]()
             cp(R("fl%d" % (k + 1)), R("sc", 15, 128, 16))
-        tt(R("b6", 0, 128), R("ac"), R("b4", 0, 128), A.subtract)
-        mm(R("b4", 0, 8), R("idb"), R("kcol"), True, False)
-        act(R("f7"), R("f4"), F.Copy, R("fl4"))
-        ts(R("b6", 256, 512), R("pp"), R("lc"), R("lc"), A.is_ge, A.mult)
-        tt(R("p31"), R("s31"), R("h31"), A.add)
-        tt(R("pw"), R("pp"), R("b6", 256, 512), A.subtract)
-        ts(R("w31"), R("p31"), R("lc"), R("lc"), A.is_ge, A.mult)
-        mm(R("b4", 0, 8), R("f7"), R("gsel", 0, 1024, 128), False, True)
-        act(R("negr", 4, 8), R("b4", 4, 8), F.Copy, None, -1.0)
-        order = (4, 5, 6, 7, 0, 1, 2, 3)
-        for k in order:
-            mm(blk("b2" if k < 4 else "b3", k % 4), blk("gsel", k), R("f7"), False, k % 4 == 3)
+        fl = R("fl4")
+        act(R("f5"), R("f4"), F.Copy, fl)
+        act(R("f6"), R("f5"), F.Copy, fl)
+        pos = R("b5", 384, 512)
+        mm(pos, rows(R("pc"), 0, 1), rows(ONE, 0, 1), True, False)
         for k in range(4, 8):
-            mm(R("b5", 0, 128), blk("lb", k), R("omi"), k == 4, False)
-        for k in order:
-            if k < 4:
-                ts(blk("cmp", k), blk("b2", k), R("b4", k, k + 1), None, A.is_gt)
+            mm(rows(pos, 32 * (k // 2), 32 * (k // 2) + 32), blk("lb", k, 32), R("omi"), False, False)
+        tt(R("pp", 0, 256, 2), R("sk"), blk("b0", 0), A.add)
+        tt(R("pp", 1, 256, 2), R("sk"), blk("b0", 1), A.add)
+        ts(R("b0", 256, 512), R("pp"), R("lc"), R("lc"), A.is_ge, A.mult)
+        ts(R("lf"), R("f6"), R("sl_"), R("bl"), A.mult, A.add, fl)
+        act(R("rt"), R("f6"), F.Identity, fl, R("sr"), R("br"))
+        begun()
+        for bank, g0, q in DIFF:
+            p = 16 * g0
+            mm(blk(bank, 0), rows(R("lf"), p, p + 16), rows(R("rt"), p, p + 16), False, False)
+            mm(blk(bank, 1), rows(R("lf"), p, p + 32), rows(R("rt"), p, p + 32), False, True)
+        tt(R("pw"), R("pp"), R("b0", 256, 512), A.subtract)
+        for bank, g0, q in DIFF:
+            if q == "V":
+                ts(R("cmp", 128 * g0, 128 * g0 + 256), R(bank, 0, 256), 0.0, None, A.is_gt)
             else:
-                act(blk("cmp", k), blk("b3", k % 4), F.Sign, None, None, R("negr", k, k + 1))
-        for k in (0, 1, 4, 5, 2, 3, 6, 7):
-            mm(R("b5", 0, 128), blk("lb", k), blk("cmp", k), False, k == 7)
-        tt(R("q31"), R("p31"), R("w31"), A.subtract)
+                act(R("cmp", 128 * g0, 128 * g0 + 256), R(bank, 0, 256), F.Sign)
+        for bank, g0, q in DIFF:
+            for k in (g0, g0 + 1):
+                mm(rows(pos, 16 * g0, 16 * g0 + 32), blk("lb", k, 32), blk("cmp", k), False, k > g0)
         cp(R("plist"), R("pw"))
-        cp(R("l31"), R("q31"))
-        tt(R("mp"), R("b5", 0, 128), MK, A.mult)
-        act(R("t4"), R("b5", 0, 128), F.Copy, None, 4095.0)
+        if t < 2:
+            for s in range(16):
+                mm(R("b4", 256, 264), band("sel", s), R("pw", 2 * s + 1, 256, 32), s == 0, s == 15)
+        tt(R("mp"), pos, R("mks"), A.mult)
+        lin(R("t4"), pos, 4095.0)
         scan(R("sp"), R("rst"), R("mp"), 0.0, A.mult, A.add)
-        ts(R("cell"), R("sp", 15, 128, 16), 0.0625, -0.46875, A.mult, A.add)
-        tt(R("vrow"), R("t4"), R("b6", 0, 128), A.add)
-        cp(R("celll"), R("cell"))
+        ts(R("celll"), R("sp", 15, 128, 16), M23, -M23, A.add, A.add)
+        tt(R("vrow"), R("t4"), R("b3", 256, 384), A.add)
         cp(R("wb", 8, 264), R("vrow"), None, R("celll"))
 
         def step(n, a, b):
@@ -455,6 +499,8 @@ def rank_program(g, core, T, topo):
                 step(n, 0, LAYS)
         act(R("lay", 0, 16 * LAYS), R(X), F.Copy, R("sl", 0, LAYS))
         cp(R("lay", 16 * LAYS, 4096), R(X), R("sl", LAYS, 256))
+        if t < 2:
+            cp(R("l31"), R("b4", 256, 264))
         to = blk(Xn, rank, MB)
 
         def kids(q, kr, a, b):
@@ -465,24 +511,32 @@ def rank_program(g, core, T, topo):
             else:
                 act(R(buf, o + 16 * a, o + 16 * b), R("lay"), F.Copy, lst)
 
-        def send(krs, buf, into, rs, ls):
-            dsts = [T.cores[(kr + rank) % N] for kr in krs]
-            ids = [DstId(rid=topo.addr(dst)[0], pnc=topo.addr(dst)[1]) for dst in dsts]
-            sync("G", [], [buf])
-            g.remote_dma_fused([RemoteDMATransfer(dst_ids=ids, dma_engine_mask=topo.mask(core, dsts[0]), srcs=[ap(buf)],
-                                                  dsts=[ap(into) for _ in krs], remote_sem=T.sem[rs])],
-                               local_sem=T.sem[ls])
+        def send(pieces, into, rs, ls):
+            sync("G", [], [buf for kr, buf in pieces])
+            n = ne if len(pieces) == 1 else ne // 4
+            calls = []
+            for k, (kr, buf) in enumerate(pieces):
+                dst = T.cores[(kr + rank) % N]
+                mask = sum(1 << x for x in topo.engines(core, dst)[n * k:n * k + n])
+                calls.append(RemoteDMATransfer(dst_ids=[DstId(rid=topo.addr(dst)[0], pnc=topo.addr(dst)[1])],
+                                               dma_engine_mask=mask, srcs=[ap(buf)], dsts=[ap(into)], remote_sem=T.sem[rs]))
+            g.remote_dma_fused(calls, local_sem=T.sem[ls])
         if t < 2:
-            lr = "lr%d" % t
-            cp(blk(lr, rank), R("lay"), R("l31"))
-            send((1, 2, 3), blk(lr, rank), blk(lr, rank), "sm%d" % t, "lq%d" % t)
-            arrive("sm%d" % t, 3 * ne, [blk(lr, r) for r in range(N) if r != rank])
-            extra.append(("lq%d" % t, ne))
-        for kr in far + near + [0]:
+            lo, xn = "lo%d" % t, "xr%d" % (t + 1)
+            cp(R(lo, 32, 128), R("lay"), R("l31", 2, 8))
+            send([(kr, blk(lo, kr, 32)) for kr in (1, 2, 3)], blk(xn, rank, 32), "sm%d" % t, "lq%d" % t)
+            cp(blk(xn, rank, 32), R("lay"), R("l31", 0, 2))
+            arrive("sm%d" % t, 3 * (ne // 4), [blk(xn, r, 32) for r in range(N) if r != rank])
+            extra.append(("lq%d" % t, 3 * (ne // 4)))
+        for kr in far + near:
             kids("V", kr, 0, 32)
             kids("S", kr, 32, 64)
-            if kr:
-                send((kr,), blk(ko, kr - 1, MB), to, "ar%d_%d" % (t, kr), "ls%d" % t)
+            send([(kr, blk(ko, kr - 1, MB))], to, "ar%d_%d" % (t, kr), "ls%d" % t)
+        if t < 2:
+            kids("S", 0, 0, 64)
+        else:
+            kids("V", 0, 0, 32)
+            kids("S", 0, 32, 64)
         extra.append(("ls%d" % t, 3 * ne))
         for kr in (1, 2, 3):
             arrive("ar%d_%d" % (t, kr), ne, [blk(Xn, (rank - kr) % N, MB)])

@@ -11,34 +11,37 @@ for _bank, _js in BANKS:
     _c = 0
     for _j in _js:
         SEG[_j] = (_bank, _c, 16 * (_j + 1))
-        _c += 16 * (_j + 1)
-BANKW = {"b2": 240, "b3": 176, "b4": 160}
-CTO = {"b2": 0, "b3": 240, "b4": 416}
+        _c += 16 * (_j + 1) + 1
+BANKW = {"b2": 242, "b3": 178, "b4": 164}
 LATE = 56
-_plan = """c16 0 0; gs 0 8; gs 8 16; gv 16 24; gv 24 32; sub 0 4; sub 4 8; d 16 24; abs 0 4; abs 4 8; neg 16 24; sub 8 12;
-sub 12 16; gv 32 40; abs 8 12; abs 12 16; ab 0 8; ab 16 24; as 24 32; ab 8 16; h 0 0; gv 40 48; as 32 40; ab 24 32;
-gv 48 56; as 40 48; ab 32 40; gv 56 64; as 48 56; ab 40 48; ab 48 56; end 0 56; neg 56 64; d 56 64; good 0 56; ab 56 64;
-end 56 64; good 56 64"""
+_plan = """c16 0 0; gs 0 8; gs 8 16; gv 16 24; gv 24 32; sub 0 4; sub 4 8; d 16 20; abs 0 4; abs 4 8; neg 16 20; sub 8 12;
+sub 12 16; gv 32 40; as 20 24; abs 8 12; abs 12 16; ab 0 8; as 24 32; ab 8 24; col 0 56; col 56 64; h 0 0; gv 40 48;
+as 32 40; ab 24 32; gv 48 56; as 40 48; ab 32 40; gv 56 60; gv 60 64; as 48 56; ab 40 48; ab 48 56; as 56 60; as 60 64;
+good 0 56; ab 56 64; good 56 64"""
 PLAN = [(w.split()[0], int(w.split()[1]), int(w.split()[2])) for w in _plan.split(";")]
-LAYS = 136
+KIDS = (((0, 0, 32, 64), (1, 0, 32, 64), (2, 0, 32, 64), (3, 0, 0, 64)),
+        ((0, 0, 26, 64), (1, 0, 32, 64), (2, 0, 32, 64), (3, 0, 0, 64)),
+        ((0, 0, 32, 64), (1, 0, 32, 64), (2, 0, 32, 64), (3, 0, 32, 64)))
+FILL = 12
+LAYS = (168, 138, 136)
 DIFF = (("b2", 0, "V"), ("b3", 4, "S"), ("b6", 2, "V"), ("b7", 6, "S"))
-M23, M28, M29 = 1.5 * 2.0 ** 23, 1.5 * 2.0 ** 28, 1.5 * 2.0 ** 29
+M23, M27, M28, M29 = (1.5 * 2.0 ** _k for _k in (23, 27, 28, 29))
 
 _f, _h, _b, _i, _u = "float32", "float16", "bfloat16", "int32", "uint16"
 _sb = {
     _b: "x0:4096 x1:4096 x2:4096 x3:4096 lay:4096 ko0:3072 ko1:3072 ko2:3072 xr0:1024 xr1:1024 xr2:1024 lo0:128 lo1:128 "
         "q16:128 bo:128 bo27:128 mk2:256 idb:128 nid:128 ldw:144 bww:144 bw:128 ones:512 omi:128 grp:256 "
-        "ca:128 cr:576 b26:128 kcl:128 dl:128 dr:256 hc:128 pc:128 ac:128 nbo:128 "
+        "ca:128 cr:144 b26:128 io:128 two:128 zz:128 c31c:8 ngrp:256 nq:128 nm:128 rneg:128 kcl:128 dl:128 dr:256 hc:128 pc:128 ac:128 nbo:128 "
         "rst:128 d:8192 ab:8192 gd:512 ej:128 ef:128 el:128 mm:128 lb:256 cmp:1024 "
-        "f0:128 f1:128 f2:128 f3:128 f4:128 f5:128 f6:128 h0:128 h1:128 h2:128 h3:128 lf:128 rt:128",
-    _h: "bo12:128 boh:128 idh:128 c16:512 ed:256",
+        "f0:128 f1:128 f2:128 f3:128 f4:128 f5:128 f6:128 h0:128 h1:128 h2:128 h3:128 lf:128 rt:128 sc:128",
+    _h: "bo12:128 boh:128 idh:128 c16:512 ed:256 sel:144 p16:128",
     _f: "wtf:1 ekt:256 kr:192 th2:512 pf:1 pm:1 pm16:1 pm4:1 pg:1 pe:1 po:1 pw2:1 gk:1 gs:1 sl_:1 bl:1 sr:1 br:1 qb:1 qb16:1 "
-        "row:144 mg:128 gi:256 bof:128 sel:144 s15:1 mks:128 i16:8 il:8 self:8 ioc:8 pl:256 kperm:128 pw3:1 tc:8 uf:8 u2:8 sq:8 "
-        "mk:512 bf:8 accf:8 sc:128 lc:1 pp:256 pw:256 mp:128 t4:128 vrow:128 sp:128 wb:264 hr:128 hf:128 "
+        "row:144 mg:128 gi:256 bof:128 selr:128 s15:1 s16:1 mks:128 pl:256 kperm:128 pw3:1 uf:8 u2:8 sq:8 "
+        "mk:512 bf:8 fst:128 lc:1 pp:256 pw:256 mp:128 t4:128 vrow:128 sp:128 wb:264 hr:128 hf:128 "
         "w1:256 ff:256",
     _i: "wti:1 kt:16 pi:1 pmi:1 pgi:1 poi:1 expi:16 ui:8 ub:8 cv:512 ci:512 best:8 jI:8 oI:8 dio:16 "
         "acc:8 fI:8 cI:8 lI:8 sk:128 si:256 sj:256",
-    _u: "expl:16 cl:512 plist:256 celll:8 l31:8 sl:256 fl0:8 fl1:8 fl2:8 fl3:8 fl4:8",
+    _u: "expl:16 cl:512 plist:256 celll:8 l31:8 c31:8 sl:256 fl0:8 fl1:8 fl2:8 fl3:8 fl4:8",
 }
 WIDTH, TYPE, PLACE, SCRATCH, _used = {}, {}, {}, {}, {}
 for _t, _list in _sb.items():
@@ -56,7 +59,7 @@ for _k in range(8):
     SCRATCH["b%d" % _k] = ("psum", [128, 512], _f)
     WIDTH["b%d" % _k], TYPE["b%d" % _k], PLACE["b%d" % _k] = 512, _f, ("b%d" % _k, 0)
 SEMAPHORES = ["qV", "qS", "qP", "qG"] + ["dl%d" % k for k in range(12)] + \
-    ["ar%d_%d" % (t, k) for t in range(3) for k in range(4)] + ["%s%d" % (s, t) for t in range(3) for s in ("ls", "lq", "sm")]
+    ["ar%d_%d" % (t, k) for t in range(3) for k in range(8)] + ["%s%d" % (s, t) for t in range(3) for s in ("ls", "lq", "sm")]
 
 
 def build_tracker(g, T):
@@ -167,8 +170,8 @@ def rank_program(g, core, T, topo):
     def sca(v):
         return ap(v) if isinstance(v, tuple) else v
 
-    def tt(out, in0, in1, op, idx=None):
-        emit("V", lambda e: e.tensor_tensor(ap(out), src(in0, idx), ap(in1), op), [out], regs(in0, in1, idx))
+    def tt(out, in0, in1, op, idx=None, oidx=None):
+        emit("V", lambda e: e.tensor_tensor(src(out, oidx), src(in0, idx), ap(in1), op), [out], regs(in0, in1, idx, oidx))
 
     def ts(out, in0, s1, s2, op0, op1=None, idx=None):
         if op1 is None:
@@ -223,7 +226,6 @@ def rank_program(g, core, T, topo):
     iota(R("q16"), [[0, 8], [1, 16]])
     iota(R("mg"), [[1, 8], [0, 16]])
     iota(R("expi"), [[1, 16]])
-    iota(R("i16"), [[16, 8]])
     iota(R("pl"), [[16, 256]])
     iota(R("kperm"), [[1, 4], [4, 32]])
     iota(R("gi"), [[1, 8], [8, 2], [0, 16]])
@@ -249,6 +251,7 @@ def rank_program(g, core, T, topo):
     ts(R("sl_"), R("pm"), 1.0, None, A.is_equal)
     ts(R("sr"), R("pm"), 0.0, None, A.is_equal)
     ts(R("s15"), R("pm"), 15.0, None, A.is_equal)
+    ts(R("s16"), R("pm"), 15.0, 0.0625, A.is_equal, A.mult)
     ts(R("gs"), R("pg"), 3.5, -0.5, A.is_gt, A.mult)
     ts(R("ldw"), R("row"), R("pe"), 4096.0, A.is_equal, A.mult)
     ts(R("idb"), ROW, R("pf"), None, A.is_equal)
@@ -258,8 +261,9 @@ def rank_program(g, core, T, topo):
     ts(top(R("ca")), top(R("q16")), top(R("pf")), None, A.is_equal)
     ts(R("bof"), R("mg"), R("pg"), None, A.is_equal)
     cp(R("expl"), R("expi"))
-    for name, v in (("kcl", 2048.0), ("b26", 2.0 ** 26), ("hc", -31.5), ("pc", -7.0)):
+    for name, v in (("kcl", 2048.0), ("hc", -31.5), ("pc", -7.0)):
         lin(top(R(name)), top(ROW), 0.0, v)
+    lin(top(R("b26")), top(ROW), 0.0, 2.0 ** 26)
     lin(R("pm16"), R("pm"), 1.0, 16.0)
     lin(R("pm4"), R("pm"), 4095.0, 4095.0)
     lin(R("qb"), R("pm"), 32.5)
@@ -270,9 +274,7 @@ def rank_program(g, core, T, topo):
     lin(R("gs"), R("gs"), 1.0, 1.0)
     lin(R("bl"), R("sr"), R("pw2"))
     lin(R("br"), R("sl_"), R("pw3"))
-    lin(R("il"), R("i16"), 1.0, R("pm"))
-    lin(R("self"), R("il"), 32.0, 4095.0 * 4096.0)
-    lin(R("ioc"), R("il"), 32.0, 1.0 - 2048.0)
+    lin(R("two"), ROW, 0.0, 2.0)
     cp(R("wtf"), R("wti"))
     tt(R("ekt"), R("kt"), R("mk2"), A.mult, R("expl"))
     ts(R("bww"), R("row"), R("pe"), R("wtf"), A.is_equal, A.mult)
@@ -281,28 +283,30 @@ def rank_program(g, core, T, topo):
     lin(R("kr"), R("b7", 0, 192), 32.0)
     for k in range(8):
         lin(R("th2", k, 512, 8), R("b7", 192, 256), 4096.0, -(2.0 ** 24))
-    ts(R("sel"), R("row"), R("pe"), R("s15"), A.is_equal, A.mult)
+    ts(R("sel"), R("row"), R("pe"), R("s16"), A.is_equal, A.mult)
     ts(R("grp"), R("gi"), R("gk"), R("gs"), A.is_equal, A.mult)
-    ts(R("b1", 256, 512), R("pl"), R("pm"), None, A.add)
-    ts(R("b1", 0, 256), R("pl"), 4095.0, R("pm4"), A.mult, A.add)
-    for name, scale in (("bw", R("wtf")), ("bo", 1.0), ("nbo", -1.0), ("bo27", 2.0 ** 27), ("bo12", 4096.0), ("boh", 1.0)):
-        ts(R(name), R("mg"), R("pg"), scale, A.is_equal, A.mult)
-    lin(R("idh"), R("idb"), 1.0)
-    lin(R("kperm"), R("kperm"), 1.0 / 128.0)
-    lin(R("omi"), R("idb"), -1.0, 1.0)
-    lin(R("mks"), MK, (1.0 - 2.0 ** -13) / 16.0)
+    ts(R("bw"), R("mg"), R("pg"), R("wtf"), A.is_equal, A.mult)
+    ts(R("idh"), ROW, R("pf"), None, A.is_equal)
     setrow(top(R("kcl")), 0, -(2.0 ** 24))
-    mid = rows(R("tc"), 32, 64)
-    iota(mid, [[16, 8]])
-    for p, v in ((32, 1.0), (34, -(2.0 ** -4)), (35, -(2.0 ** -16))):
+    iota(R("zz"), [[0, 128]])
+    select(top(R("cr", 0, 128)), top(R("b26")), [[1, 128]], A.is_ge, 0.0, -112, -1)
+    iota(top(R("cr", 128, 129)), [[0, 1]])
+    mid, own, lhs = (rows(r, 32, 64) for r in (R("cr", 0, 128), R("cr", 128, 129), R("ca")))
+    iota(mid, [[0, 128]], 0, 1)
+    select(own, rows(R("ones", 0, 1), 32, 64), [[0, 1]], A.is_gt, -(2.0 ** -22), 0, 0)
+    for p, v, w in ((32, -(2.0 ** 27), 32.0), (33, 2.0 ** 23, 2.0 ** 24), (34, 0.0, -4096.0)):
         setrow(mid, p, v)
-    lin(mid, mid, -(2.0 ** 27))
-    select(rows(R("ca"), 32, 64), rows(R("q16"), 32, 64), [[0, 128]], A.is_equal, 1.0, 0, 1)
-    for j in range(8):
-        bank, c, w = SEG[j]
-        piece = R("cr", CTO[bank] + c, CTO[bank] + c + w)
-        lin(rows(piece, 32, 64), rows(R("ones", 0, w), 32, 64), rows(R("tc", j, j + 1), 32, 64))
-        select(top(piece), top(R("b26", 0, w)), [[1, w]], A.is_ge, 0.0, -16 * j, -1)
+        setrow(own, p, w)
+    select(lhs, rows(R("q16"), 32, 64), [[0, 128]], A.is_equal, 1.0, 0, 1)
+    select(lhs, lhs, [[0, 128]], A.is_ge, -(2.0 ** 31), 2, -1)
+    select(R("omi"), ONE, [[-1, 128]], A.not_equal, 0.0, 0, 1)
+    select(R("rneg"), R("zz"), [[0, 8], [1, 16]], A.not_equal, -(2.0 ** 21), 0, 0)
+    select(top(R("nm")), top(R("zz")), [[0, 8], [1, 16]], A.is_equal, -(2.0 ** 20), 0, -1)
+    iota(top(R("nq")), [[0, 8], [-1, 16]])
+    iota(top(R("c31c")), [[0, 8]], 0, 128)
+    setrow(top(R("c31c")), 1, -7.5 / 16)
+    iota(top(R("io")), [[32, 128]])
+    setrow(top(R("io")), 1, 1.0)
     iota(top(R("dl")), [[1, 128]])
     setrow(top(R("dl")), 0, 1.0)
     for k, w in enumerate((1, 16384)):
@@ -310,11 +314,21 @@ def rank_program(g, core, T, topo):
         setrow(top(blk("dr", k)), 1, -float(w))
     iota(top(R("ac")), [[32, 128]])
     setrow(top(R("ac")), 1, 28672.0)
-    setrow(top(R("ac")), 2, 25.0)
+    setrow(top(R("ac")), 2, -7.0)
+
+    def later_constants():
+        for name, scale in (("bo27", 2.0 ** 27), ("bo12", 4096.0), ("boh", 1.0), ("bo", 1.0), ("nbo", -1.0)):
+            lin(R(name), R("bof"), scale)
+        lin(R("ngrp"), R("grp"), -1.0)
+        lin(R("kperm"), R("kperm"), 1.0 / 128.0)
+        lin(R("mks"), MK, (1.0 - 2.0 ** -13) / 16.0)
+        lin(R("selr"), R("bof"), R("s15"))
+        lin(R("b1", 256, 512), R("pl"), 1.0, R("pm"))
+        lin(R("b1", 0, 256), R("pl"), 4095.0, R("pm4"))
 
     extra = []
     ne = len(topo.engines(core, T.cores[(rank + 1) % N]))
-    far = [kr for kr in (1, 2, 3) if topo.die(T.cores[(kr + rank) % N]) != topo.die(core)]
+    far = [kr for kr in (2, 1, 3) if topo.die(T.cores[(kr + rank) % N]) != topo.die(core)]
     near = [kr for kr in (1, 2, 3) if kr not in far]
 
     for t in range(3):
@@ -322,6 +336,7 @@ def rank_program(g, core, T, topo):
         Xn = "x%d" % (t + 1)
         ko = "ko%d" % t
         xr = "xr%d" % t
+        early = t == 0
 
         def last(a, st):
             return R(xr, a, 128, st) if t else R(X, 32 * a + 31, 4096, 32 * st)
@@ -356,6 +371,7 @@ def rank_program(g, core, T, topo):
         for what, m0, m1 in PLAN:
             d, ab, lst = wide("d", m0, m1), wide("ab", m0, m1), R("cl", 8 * m0, 8 * m1)
             bank = R("b%d" % (6 + m0 // 4 % 2), 0, 128 * (m1 - m0))
+            out = R("b5", 8 * (m0 - LATE), 8 * (m1 - LATE)) if m0 >= LATE else R("b0", 8 * m0, 8 * m1)
             if what == "gs":
                 act(d, R(X), F.Copy, lst)
             elif what == "sub":
@@ -370,114 +386,123 @@ def rank_program(g, core, T, topo):
             elif what == "neg":
                 ts(ab, d, 0.0, -2.0, A.min, A.mult)
             elif what in ("d", "ab"):
-                out = R("b5", 8 * (m0 - LATE), 8 * (m1 - LATE)) if m0 >= LATE else R("b0", 8 * m0, 8 * m1)
                 for s in range(16):
-                    mm(out, band("ldw", s), R(what, 128 * m0 + s, 128 * m1, 16), False, False)
+                    mm(out, band("ldw", s), R(what, 128 * m0 + s, 128 * m1, 16), False, m1 in (LATE, 64) and s == 15)
             elif what == "c16":
                 ts(R("c16"), R("cl"), -2048.0, None, A.add)
-            elif what == "end":
-                mm(R("b5" if m0 else "b0", 0, 8 * (m1 - m0)), R("idh"), R("c16", 8 * m0, 8 * m1), False, True)
+            elif what == "col":
+                mm(out, R("idh"), R("c16", 8 * m0, 8 * m1), False, False)
             elif what == "good":
                 good("b5" if m0 else "b0", 8 * m0, 8 * m1)
             else:
                 mm(R("b6", 0, 128), rows(R("hc"), 0, 1), rows(ONE, 0, 1), True, False)
                 for k in range(4):
                     mm(blk("b6", k, 32), R("bw"), last(k, 4), False, k == 3)
+        if t == 0:
+            later_constants()
         for bank, js in BANKS:
-            mm(R(bank, 0, BANKW[bank]), rows(R("ca"), 0, 36), rows(R("cr", CTO[bank], CTO[bank] + BANKW[bank]), 0, 36),
-               True, False)
+            mm(R(bank, 0, BANKW[bank]), rows(R("zz"), 0, 1), rows(R("ones", 0, BANKW[bank]), 0, 1), True, False)
+        for j in range(8):
+            bank, c, w = SEG[j]
+            mm(R(bank, c, c + w + 1), rows(R("ca"), 0, 35 + j), rows(R("cr", 128 - w, 129), 0, 35 + j), False, False)
         for k in range(8):
-            red(R("bf", k, k + 1), R("mk", k, 512, 8), A.min)
-        cp(R("best"), R("bf"))
-        ts(R("dio", 0, 8), R("bf"), 2.0 ** -12, 2047.5 + 2.0 ** -13, A.mult, A.add)
+            red(R("best", k, k + 1), R("mk", k, 512, 8), A.min)
         ts(R("jI"), R("best"), 5, 127, A.arith_shift_right, A.bitwise_and)
-        ts(R("oI"), R("best"), 1, 15, A.arith_shift_right, A.bitwise_and)
+        ts(R("dio", 0, 8), R("best"), 2.0 ** -12, 2047.5 + 2.0 ** -13, A.mult, A.add)
+        ts(R("dio", 8, 16), R("best"), 1, 15, A.arith_shift_right, A.bitwise_and)
         tt(R("ej"), R("jI"), MK, A.mult, E8)
-        tt(R("dio", 8, 16), R("oI"), R("ioc"), A.add)
         tt(R("ed"), R("dio"), R("mk2"), A.mult, R("expl"))
         ts(R("hr"), R("b6", 0, 128), M29, -M29, A.add, A.add)
         tt(R("hf"), R("b6", 0, 128), R("hr"), A.subtract)
         lin(blk("b0", 0), R("hf"), R("pm"), R("qb"))
         lin(blk("b0", 1), R("hf"), R("pm16"), R("qb16"))
         seg = {j: R(SEG[j][0], SEG[j][1], SEG[j][1] + SEG[j][2]) for j in range(8)}
-        for bank, js in BANKS:
+        for part, js in (("target", (7, 6, 5, 4)), ("key", (7, 6, 5, 4)), ("target", (3, 2, 1, 0)), ("key", (3, 2, 1, 0))):
             for j in js:
-                mm(seg[j], R("bo27"), R("ej", 0, SEG[j][2]), False, False)
-        for bank, js in BANKS:
-            for j in js:
-                mm(seg[j], R("bo12"), R("ed", 0, SEG[j][2]), False, False)
-                mm(seg[j], R("boh"), R("ed", 128, 128 + SEG[j][2]), False, j == js[-1])
-        for bank, js in BANKS:
-            for j in js:
-                red(R("accf", j, j + 1), seg[j], A.min, True)
-        tt(R("acc"), R("accf"), R("self"), A.min)
+                w = SEG[j][2]
+                if part == "target":
+                    mm(seg[j], R("bo27"), R("ej", 0, w), False, False)
+                    mm(seg[j], rows(ONE, 0, 2), rows(R("io", 0, w), 0, 2), False, False)
+                else:
+                    mm(seg[j], R("bo12"), R("ed", 0, w), False, False)
+                    mm(seg[j], R("boh"), R("ed", 128, 128 + w), False, j in (6, 4, 0))
+        for j in range(7, -1, -1):
+            red(R("acc", j, j + 1), R(SEG[j][0], SEG[j][1], SEG[j][1] + 1 + SEG[j][2]), A.min, True)
         ts(R("fI"), R("acc"), 5, 127, A.arith_shift_right, A.bitwise_and)
         ts(R("cI"), R("acc"), 31, None, A.bitwise_and)
         tt(R("ef"), R("fI"), MK, A.mult, E8)
         mm(R("b5", 0, 128), R("bo"), R("ef"), True, True)
         cp(R("fl0"), R("fI"))
         act(R("f0"), R("b5", 0, 128), F.Copy)
-        ts(R("lI"), R("cI"), -1.0, 32.0, A.mult, A.add)
-        tt(R("el"), R("lI"), MK, A.mult, E8)
-        mm(R("b4", 0, 128), R("bo"), R("el"), True, True)
-        mm(R("b5", 128, 384), R("el"), R("grp"), True, True)
+        tt(R("el"), R("cI"), MK, A.mult, E8)
+        mm(R("b4", 0, 128), rows(R("two"), 0, 16), rows(ONE, 0, 16), True, False)
+        mm(R("b4", 0, 128), R("nbo"), R("el"), False, True)
+        mm(R("b5", 128, 384), R("two"), R("grp"), True, False)
+        mm(R("b5", 128, 384), R("el"), R("ngrp"), False, True)
         mm(R("b3", 256, 384), rows(ONE, 0, 3), rows(R("ac"), 0, 3), True, False)
-        mm(R("b3", 256, 384), R("nbo"), R("el"), False, True)
+        mm(R("b3", 256, 384), R("bo"), R("el"), False, True)
         for bank, g0, q in DIFF:
             mm(R(bank, 0, 256), rows(R("dl"), 0, 2), rows(R("dr"), 0, 2), True, False)
         begun = fence()
         gaps = [
             lambda: red(R("lc"), R("b4", 0, 128), A.add),
             lambda: ts(R("sk"), R("kperm"), R("lc"), -63.5 / 128.0, A.mult, A.add),
-            lambda: None,
-            lambda: None,
+            lambda: tt(R("pp", 0, 256, 2), R("sk"), blk("b0", 0), A.add),
+            lambda: tt(R("pp", 1, 256, 2), R("sk"), blk("b0", 1), A.add),
         ]
         for k in range(4):
             fl = R("fl%d" % k)
             tt(R("mm"), R("f%d" % k), MK, A.mult, fl)
             act(R("h%d" % k), R("f%d" % k), F.Copy, fl)
             act(R("f%d" % (k + 1)), R("h%d" % k), F.Copy, fl)
-            if k == 0:
-                act(R("lb"), R("b5", 128, 384), F.Copy)
             scan(R("sc"), R("rst"), R("mm"), 0.0, A.mult, A.add)
             gaps[k]()
             cp(R("fl%d" % (k + 1)), R("sc", 15, 128, 16))
         fl = R("fl4")
         act(R("f5"), R("f4"), F.Copy, fl)
         act(R("f6"), R("f5"), F.Copy, fl)
-        pos = R("b5", 384, 512)
+        pos = R("b4", 384, 512)
         mm(pos, rows(R("pc"), 0, 1), rows(ONE, 0, 1), True, False)
-        for k in range(4, 8):
-            mm(rows(pos, 32 * (k // 2), 32 * (k // 2) + 32), blk("lb", k, 32), R("omi"), False, False)
-        tt(R("pp", 0, 256, 2), R("sk"), blk("b0", 0), A.add)
-        tt(R("pp", 1, 256, 2), R("sk"), blk("b0", 1), A.add)
         ts(R("b0", 256, 512), R("pp"), R("lc"), R("lc"), A.is_ge, A.mult)
+        tt(R("pw"), R("pp"), R("b0", 256, 512), A.subtract)
+        if early:
+            mm(R("b0", 0, 128), rows(R("nq"), 0, 1), rows(ONE, 0, 1), True, False)
+            mm(R("b0", 0, 128), R("selr"), R("pw", 1, 256, 2), False, True)
         ts(R("lf"), R("f6"), R("sl_"), R("bl"), A.mult, A.add, fl)
         act(R("rt"), R("f6"), F.Identity, fl, R("sr"), R("br"))
+        act(R("lb"), R("b5", 128, 384), F.Copy)
         begun()
         for bank, g0, q in DIFF:
             p = 16 * g0
             mm(blk(bank, 0), rows(R("lf"), p, p + 16), rows(R("rt"), p, p + 16), False, False)
             mm(blk(bank, 1), rows(R("lf"), p, p + 32), rows(R("rt"), p, p + 32), False, True)
-        tt(R("pw"), R("pp"), R("b0", 256, 512), A.subtract)
+        for k in range(4, 8):
+            mm(rows(pos, 32 * (k // 2), 32 * (k // 2) + 32), blk("lb", k, 32), R("omi"), False, False)
+        if early:
+            ts(R("hr"), R("b0", 0, 128), M27, -M27, A.add, A.add)
         for bank, g0, q in DIFF:
             if q == "V":
                 ts(R("cmp", 128 * g0, 128 * g0 + 256), R(bank, 0, 256), 0.0, None, A.is_gt)
             else:
                 act(R("cmp", 128 * g0, 128 * g0 + 256), R(bank, 0, 256), F.Sign)
+        lin(R("fst"), R("b3", 256, 384), 1.0)
         for bank, g0, q in DIFF:
             for k in (g0, g0 + 1):
                 mm(rows(pos, 16 * g0, 16 * g0 + 32), blk("lb", k, 32), blk("cmp", k), False, k > g0)
-        cp(R("plist"), R("pw"))
         if t < 2:
+            lin(R("p16"), R("pw", 1, 256, 2), 1.0, -2048.0)
+            mm(R("b5", 0, 8), rows(ONE, 0, 2), rows(R("c31c"), 0, 2), True, False)
             for s in range(16):
-                mm(R("b4", 256, 264), band("sel", s), R("pw", 2 * s + 1, 256, 32), s == 0, s == 15)
+                mm(R("b5", 0, 8), band("sel", s), R("p16", s, 128, 16), False, s == 15)
+        if early:
+            tt(R("hf"), R("b0", 0, 128), R("hr"), A.is_equal)
+            mm(R("b2", 0, 128), rows(R("ca"), 0, 16), rows(R("nm"), 0, 16), True, False)
+        cp(R("plist"), R("pw"))
         tt(R("mp"), pos, R("mks"), A.mult)
         lin(R("t4"), pos, 4095.0)
         scan(R("sp"), R("rst"), R("mp"), 0.0, A.mult, A.add)
         ts(R("celll"), R("sp", 15, 128, 16), M23, -M23, A.add, A.add)
-        tt(R("vrow"), R("t4"), R("b3", 256, 384), A.add)
-        cp(R("wb", 8, 264), R("vrow"), None, R("celll"))
+        tt(R("wb", 8, 264), R("t4"), R("fst"), A.add, None, R("celll"))
 
         def step(n, a, b):
             if n == 0:
@@ -492,16 +517,16 @@ def rank_program(g, core, T, topo):
                 ts(R("sj", a, b), R("si", a, b), 4095, None, A.bitwise_and)
             else:
                 cp(R("sl", a, b), R("sj", a, b))
-        for n, second in ((0, 0), (0, 1), (1, 0), (1, 1), (2, 0), (3, 0), (2, 1), (4, 0), (3, 1), (5, 0), (4, 1), (5, 1)):
+        cut = LAYS[t]
+        for n, second in ((0, 0), (0, 1), (1, 0), (1, 1), (2, 0), (3, 0), (2, 1), (4, 0), (3, 1), (5, 0), (4, 1)):
             if second:
-                step(n, LAYS, 256)
+                step(n, cut, 256)
             else:
-                step(n, 0, LAYS)
-        act(R("lay", 0, 16 * LAYS), R(X), F.Copy, R("sl", 0, LAYS))
-        cp(R("lay", 16 * LAYS, 4096), R(X), R("sl", LAYS, 256))
-        if t < 2:
-            cp(R("l31"), R("b4", 256, 264))
-        to = blk(Xn, rank, MB)
+                step(n, 0, cut)
+            if n == 5 and early:
+                ts(R("c31"), R("b5", 0, 8), M23, -M23, A.add, A.add)
+        mine = cut - FILL if early else cut
+        act(R("lay", 0, 16 * mine), R(X), F.Copy, R("sl", 0, mine))
 
         def kids(q, kr, a, b):
             buf, o = (ko, MB * (kr - 1)) if kr else (Xn, MB * rank)
@@ -521,26 +546,46 @@ def rank_program(g, core, T, topo):
                 calls.append(RemoteDMATransfer(dst_ids=[DstId(rid=topo.addr(dst)[0], pnc=topo.addr(dst)[1])],
                                                dma_engine_mask=mask, srcs=[ap(buf)], dsts=[ap(into)], remote_sem=T.sem[rs]))
             g.remote_dma_fused(calls, local_sem=T.sem[ls])
-        if t < 2:
+
+        def ahead(window):
             lo, xn = "lo%d" % t, "xr%d" % (t + 1)
-            cp(R(lo, 32, 128), R("lay"), R("l31", 2, 8))
+            cp(R(lo, 32, 128), window, R("l31", 2, 8))
             send([(kr, blk(lo, kr, 32)) for kr in (1, 2, 3)], blk(xn, rank, 32), "sm%d" % t, "lq%d" % t)
-            cp(blk(xn, rank, 32), R("lay"), R("l31", 0, 2))
+            cp(blk(xn, rank, 32), window, R("l31", 0, 2))
             arrive("sm%d" % t, 3 * (ne // 4), [blk(xn, r, 32) for r in range(N) if r != rank])
             extra.append(("lq%d" % t, 3 * (ne // 4)))
-        for kr in far + near:
-            kids("V", kr, 0, 32)
-            kids("S", kr, 32, 64)
-            send([(kr, blk(ko, kr - 1, MB))], to, "ar%d_%d" % (t, kr), "ls%d" % t)
-        if t < 2:
-            kids("S", 0, 0, 64)
+        if early:
+            tt(R("vrow"), R("sj"), R("hf"), A.mult, R("c31"))
+            mm(R("b2", 0, 128), R("bof"), R("vrow"), False, True)
+            step(5, cut, 256)
+            cp(R("lay", 16 * mine, 16 * cut), R(X), R("sl", mine, cut))
+            scan(R("sp"), R("rneg"), R("b2", 0, 128), 0.0, A.add, A.max)
+            cp(R("l31"), R("sp", 15, 128, 16))
+            ahead(R(X))
         else:
-            kids("V", 0, 0, 32)
-            kids("S", 0, 32, 64)
-        extra.append(("ls%d" % t, 3 * ne))
-        for kr in (1, 2, 3):
-            arrive("ar%d_%d" % (t, kr), ne, [blk(Xn, (rank - kr) % N, MB)])
-    for kr in [0] + [(-k) % N for k in far + near]:
-        s = (rank - kr) % N
-        dma("Y", T.y[:, MB * s:MB * s + MB], T.x3[:, MB * s:MB * s + MB], [], [blk("x3", s, MB)])
+            step(5, cut, 256)
+            if t < 2:
+                ts(R("l31"), R("b5", 0, 8), 16.0, 7.5, A.mult, A.add)
+        cp(R("lay", 16 * cut, 4096), R(X), R("sl", cut, 256))
+        if t < 2 and not early:
+            ahead(R("lay"))
+        order = far + near + [0]
+        landed = []
+        for n, (k, a, m, b) in enumerate(KIDS[t]):
+            kr = order[k]
+            if m > a:
+                kids("V", kr, a, m)
+            kids("S", kr, m, b)
+            if kr:
+                o = MB * (kr - 1)
+                send([(kr, R(ko, o + 16 * a, o + 16 * b))], R(Xn, MB * rank + 16 * a, MB * rank + 16 * b),
+                     "ar%d_%d" % (t, n), "ls%d" % t)
+            s = (rank + kr) % N
+            landed.append((k, R(Xn, MB * s + 16 * a, MB * s + 16 * b)))
+        for n, (k, r) in enumerate(landed):
+            if k < 3:
+                arrive("ar%d_%d" % (t, n), ne, [r])
+        extra.append(("ls%d" % t, ne * sum(k < 3 for k, r in landed)))
+    for k, r in landed:
+        dma("Y" if k < 3 else "S", T.y[:, r[1]:r[2]], ap(r), [], [r])
     finish(extra)

from concourse.bass import DstId, RemoteDMATransfer
from concourse.mybir import AluOpType, AxisListType, ActivationFunctionType

A = AluOpType
F = ActivationFunctionType
N = 4
MB = 1024
BANKS = (("b2", (7, 6)), ("b3", (5, 4)), ("b4", (3, 2, 1, 0)))
SEG = {}
for _bank, _js in BANKS:
    _c = 0
    for _j in _js:
        SEG[_j] = (_bank, _c, 16 * (_j + 1))
        _c += 16 * (_j + 1) + 1
BANKW = {"b2": 242, "b3": 178, "b4": 164}
LATE = 56
_plan = """c16 0 0; gs 0 8; gs 8 16; gv 16 24; gv 24 32; sub 0 4; sub 4 8; d 16 20; abs 0 4; abs 4 8; neg 16 20; sub 8 12;
sub 12 16; gv 32 40; as 20 24; abs 8 12; abs 12 16; ab 0 8; as 24 32; ab 8 24; col 0 56; col 56 64; h 0 0; gv 40 48;
as 32 40; ab 24 32; gv 48 56; as 40 48; ab 32 40; gv 56 60; gv 60 64; as 48 56; ab 40 48; ab 48 56; as 56 60; as 60 64;
good 0 56; ab 56 64; good 56 64"""
PLAN = [(w.split()[0], int(w.split()[1]), int(w.split()[2])) for w in _plan.split(";")]
KIDS = (((0, 0, 32, 64), (1, 0, 32, 64), (2, 0, 32, 64), (3, 0, 0, 64)),
        ((0, 0, 26, 64), (1, 0, 32, 64), (2, 0, 32, 64), (3, 0, 0, 64)),
        ((0, 0, 32, 64), (1, 0, 32, 64), (2, 0, 32, 64), (3, 0, 32, 64)))
FILL = 12
LAYS = (168, 138, 136)
DIFF = (("b2", 0, "V"), ("b3", 4, "S"), ("b6", 2, "V"), ("b7", 6, "S"))
M23, M27, M28, M29 = (1.5 * 2.0 ** _k for _k in (23, 27, 28, 29))

_f, _h, _b, _i, _u = "float32", "float16", "bfloat16", "int32", "uint16"
_sb = {
    _b: "x0:4096 x1:4096 x2:4096 x3:4096 lay:4096 ko0:3072 ko1:3072 ko2:3072 xr0:1024 xr1:1024 xr2:1024 lo0:128 lo1:128 "
        "q16:128 bo:128 bo27:128 mk2:256 idb:128 nid:128 ldw:144 bww:144 bw:128 ones:512 omi:128 grp:256 "
        "ca:128 cr:144 b26:128 io:128 two:128 zz:128 c31c:8 ngrp:256 nq:128 nm:128 rneg:128 kcl:128 dl:128 dr:256 hc:128 pc:128 ac:128 nbo:128 "
        "rst:128 d:8192 ab:8192 gd:512 ej:128 ef:128 el:128 mm:128 lb:256 cmp:1024 "
        "f0:128 f1:128 f2:128 f3:128 f4:128 f5:128 f6:128 h0:128 h1:128 h2:128 h3:128 lf:128 rt:128 sc:128",
    _h: "bo12:128 boh:128 idh:128 c16:512 ed:256 sel:144 p16:128",
    _f: "wtf:1 ekt:256 kr:192 th2:512 pf:1 pm:1 pm16:1 pm4:1 pg:1 pe:1 po:1 pw2:1 gk:1 gs:1 sl_:1 bl:1 sr:1 br:1 qb:1 qb16:1 "
        "row:144 mg:128 gi:256 bof:128 selr:128 s15:1 s16:1 mks:128 pl:256 kperm:128 pw3:1 uf:8 u2:8 sq:8 "
        "mk:512 bf:8 fst:128 lc:1 pp:256 pw:256 mp:128 t4:128 vrow:128 sp:128 wb:264 hr:128 hf:128 "
        "w1:256 ff:256",
    _i: "wti:1 kt:16 pi:1 pmi:1 pgi:1 poi:1 expi:16 ui:8 ub:8 cv:512 ci:512 best:8 jI:8 oI:8 dio:16 "
        "acc:8 fI:8 cI:8 lI:8 sk:128 si:256 sj:256",
    _u: "expl:16 cl:512 plist:256 celll:8 l31:8 c31:8 sl:256 fl0:8 fl1:8 fl2:8 fl3:8 fl4:8",
}
WIDTH, TYPE, PLACE, SCRATCH, _used = {}, {}, {}, {}, {}
for _t, _list in _sb.items():
    for _e in _list.split():
        _k, _w = _e.split(":")
        WIDTH[_k], TYPE[_k], PLACE[_k] = int(_w), _t, (_k, 0)
        if int(_w) <= 16 and _k not in ("wti", "kt"):
            PLACE[_k] = ("small_" + _t, _used.get(_t, 0))
            _used[_t] = _used.get(_t, 0) + 16
        else:
            SCRATCH[_k] = ("sbuf", [128, int(_w)], _t)
for _k, _v in _used.items():
    SCRATCH["small_" + _k] = ("sbuf", [128, _v], _k)
for _k in range(8):
    SCRATCH["b%d" % _k] = ("psum", [128, 512], _f)
    WIDTH["b%d" % _k], TYPE["b%d" % _k], PLACE["b%d" % _k] = 512, _f, ("b%d" % _k, 0)
SEMAPHORES = ["qV", "qS", "qP", "qG"] + ["dl%d" % k for k in range(12)] + \
    ["ar%d_%d" % (t, k) for t in range(3) for k in range(8)] + ["%s%d" % (s, t) for t in range(3) for s in ("ls", "lq", "sm")]


def build_tracker(g, T):
    eng = {"V": g.vector, "S": g.scalar, "P": g.tensor, "G": g, "Y": g.sync}
    cnt = {"V": 0, "S": 0, "P": 0, "G": 0}
    clk = {q: {} for q in eng}
    snap = {}
    acc = {}
    ndma = [0]
    base = [0]

    def meet(r, e):
        if r[1] >= e[3] or e[2] >= r[2]:
            return False
        return not (r[3] == e[4] and r[3] > 1 and (r[1] - e[2]) % r[3])

    def sync(q, outs, ins):
        need = {}
        for w, regs in ((True, outs), (False, ins)):
            for r in regs:
                psum = SCRATCH[r[0]][0] == "psum"
                for e in acc.get(r[0], ()):
                    hit = (psum and e[0] != q) or ((w or e[5]) and (q, e[0]) != ("P", "P") and meet(r, e))
                    tok = e[1]
                    if hit and clk[q].get(tok[0], 0) < tok[1] and need.get(tok[0], 0) < tok[1]:
                        need[tok[0]] = tok[1]
        items = sorted(need.items(), key=lambda kv: kv[0])
        for s, v in items:
            if not any(s2 != s and snap[(s2, v2)].get(s, 0) >= v for s2, v2 in items):
                eng[q].wait_ge(T.sem[s], v)
        for tok in items:
            for s, v in snap[tok].items():
                clk[q][s] = max(v, clk[q].get(s, 0))

    def note(q, tok, outs, ins):
        for w, regs in ((True, outs), (False, ins)):
            for r in regs:
                lst = acc.setdefault(r[0], [])
                lst[:] = [e for e in lst if not (e[0] == q and (e[5] == w or w) and e[2] >= r[1] and e[3] <= r[2]
                                                 and (r[3] == 1 or (e[4] == r[3] and (e[2] - r[1]) % r[3] == 0)))]
                lst.append((q, tok, r[1], r[2], r[3], w))

    def done(q, who, tok, outs, ins):
        snap[tok] = dict(clk[q]) if q else {}
        snap[tok][tok[0]] = tok[1]
        note(who, tok, outs, ins)

    def emit(q, call, outs, ins):
        sync(q, outs, ins)
        if q == "G":
            if outs[0][4] != base[0] and clk[q].get("qG", 0) < cnt[q]:
                g.wait_ge(T.sem["qG"], cnt[q])
                clk[q]["qG"] = cnt[q]
            base[0] = outs[0][4]
        cnt[q] += 1
        call(eng[q]).then_inc(T.sem["q" + q], 1)
        done(q, q, ("q" + q, cnt[q]), outs, ins)

    def dma(q, out_ap, in_ap, outs, ins):
        sync(q, outs, ins)
        s = "dl%d" % ndma[0]
        ndma[0] += 1
        eng[q].dma_start(out_ap, in_ap).then_inc(T.sem[s], 16)
        done(q, s, (s, 16), outs, ins)

    def arrive(s, val, outs):
        done(None, s, (s, val), outs, ())

    def fence():
        n = cnt["P"]
        return lambda: g.tensor.wait_ge(T.sem["qP"], n)

    def finish(extra):
        for q in ("V", "S", "P", "G"):
            g.wait_ge(T.sem["q" + q], cnt[q])
        for k in range(ndma[0]):
            g.wait_ge(T.sem["dl%d" % k], 16)
        for s, v in extra:
            g.wait_ge(T.sem[s], v)
    return emit, dma, sync, arrive, fence, finish


def rank_program(g, core, T, topo):
    rank = T.rank_of(core)
    if rank is None:
        return
    emit, dma, sync, arrive, fence, finish = build_tracker(g, T)

    def R(name, a=0, b=None, st=1):
        p, o = PLACE[name]
        return (p, o + a, o + (WIDTH[name] if b is None else b), st, 0, 128)

    def blk(name, k, w=128):
        return R(name, w * k, w * k + w)

    def rows(r, p0, p1):
        return r[:4] + (p0, p1)

    def ap(r):
        return T[r[0]][r[4]:r[5], r[1]:r[2]:r[3]] if r[3] > 1 else T[r[0]][r[4]:r[5], r[1]:r[2]]

    def src(r, idx):
        return ap(r) if idx is None else ap(r).indirect(ap(idx))

    def regs(*rs):
        return [r for r in rs if isinstance(r, tuple)]

    def sca(v):
        return ap(v) if isinstance(v, tuple) else v

    def tt(out, in0, in1, op, idx=None, oidx=None):
        emit("V", lambda e: e.tensor_tensor(src(out, oidx), src(in0, idx), ap(in1), op), [out], regs(in0, in1, idx, oidx))

    def ts(out, in0, s1, s2, op0, op1=None, idx=None):
        if op1 is None:
            emit("V", lambda e: e.tensor_scalar(ap(out), ap(in0), sca(s1), None, op0), [out], regs(in0, s1))
        else:
            emit("V", lambda e: e.tensor_scalar(ap(out), src(in0, idx), sca(s1), sca(s2), op0, op1), [out],
                 regs(in0, s1, s2, idx))

    def cp(out, in_, idx=None, oidx=None):
        emit("V", lambda e: e.tensor_copy(src(out, oidx), src(in_, idx)), [out], regs(in_, idx, oidx))

    def fill(out, v):
        emit("V", lambda e: e.memset(ap(out), v), [out], [])

    def red(out, in_, op, absv=False):
        emit("V", lambda e: e.tensor_reduce(ap(out), ap(in_), AxisListType.X, op, apply_absolute_value=absv), [out], [in_])

    def scan(out, d0, d1, init, op0, op1):
        emit("V", lambda e: e.tensor_tensor_scan(ap(out), ap(d0), ap(d1), sca(init), op0, op1), [out], regs(d0, d1, init))

    def act(out, in_, fn, idx=None, scale=None, bias=None):
        kw = {}
        if scale is not None:
            kw["scale"] = sca(scale)
        if bias is not None:
            kw["bias"] = sca(bias)
        emit("S", lambda e: e.activation(ap(out), src(in_, idx), fn, **kw), [out], regs(in_, idx, scale, bias))

    def mm(out, lhsT, rhs, start, stop):
        emit("P", lambda e: e.matmul(ap(out), ap(lhsT), ap(rhs), start, stop), [out], [lhsT, rhs])

    def iota(out, pattern, cm=0, base=0):
        kw = {} if out[0].endswith(_i) else {"allow_small_or_imprecise_dtypes": True}
        emit("G", lambda e: e.iota(ap(out), pattern, base, cm, **kw), [out], [])

    def select(out, in_, pattern, op, other, base, cm):
        emit("G", lambda e: e.affine_select(ap(out), ap(in_), pattern, op, other, base, cm), [out], [in_])

    def setrow(r, p, v):
        select(r, r, [[0, r[2] - r[1]]], A.not_equal, v, r[4] - p, 1)

    def band(name, s):
        return R(name, 15 - s, 143 - s)

    dma("S", T.wti[:], T.wt[:], [R("wti")], [])
    dma("Y", T.kt[:, 0:12], T.km[:], [R("kt", 0, 12)], [])
    dma("Y", T.kt[:, 12:16], T.th[:], [R("kt", 12, 16)], [])
    dma("Y", T.x0[:], T.gen0[:], [R("x0")], [])

    iota(R("pi"), [[0, 1]], 1)
    iota(R("row"), [[1, 144]])
    iota(R("q16"), [[0, 8], [1, 16]])
    iota(R("mg"), [[1, 8], [0, 16]])
    iota(R("expi"), [[1, 16]])
    iota(R("pl"), [[16, 256]])
    iota(R("kperm"), [[1, 4], [4, 32]])
    iota(R("gi"), [[1, 8], [8, 2], [0, 16]])
    MK = R("mk2", 0, 128)
    E8 = R("expl", 0, 8)
    ROW = R("row", 0, 128)
    ONE = R("ones", 0, 128)

    def top(r):
        return rows(r, 0, 32)

    def lin(out, in_, scale, bias=0.0):
        act(out, in_, F.Identity, None, scale, bias)
    ts(R("pmi"), R("pi"), 15, None, A.bitwise_and)
    ts(R("pgi"), R("pi"), 4, None, A.arith_shift_right)
    cp(R("pf"), R("pi"))
    cp(R("pm"), R("pmi"))
    cp(R("pg"), R("pgi"))
    ts(R("poi"), R("pgi"), 1, None, A.bitwise_and)
    fill(R("ones"), 1.0)
    ts(R("pe"), R("pg"), 16.0, 15.0, A.mult, A.add)
    cp(R("po"), R("poi"))
    ts(R("sl_"), R("pm"), 1.0, None, A.is_equal)
    ts(R("sr"), R("pm"), 0.0, None, A.is_equal)
    ts(R("s15"), R("pm"), 15.0, None, A.is_equal)
    ts(R("s16"), R("pm"), 15.0, 0.0625, A.is_equal, A.mult)
    ts(R("gs"), R("pg"), 3.5, -0.5, A.is_gt, A.mult)
    ts(R("ldw"), R("row"), R("pe"), 4096.0, A.is_equal, A.mult)
    ts(R("idb"), ROW, R("pf"), None, A.is_equal)
    ts(MK, R("q16"), R("pm"), None, A.is_equal)
    ts(R("mk2", 128, 256), R("q16"), R("pm"), None, A.is_equal)
    ts(R("rst"), R("q16"), 0.0, None, A.is_gt)
    ts(top(R("ca")), top(R("q16")), top(R("pf")), None, A.is_equal)
    ts(R("bof"), R("mg"), R("pg"), None, A.is_equal)
    cp(R("expl"), R("expi"))
    for name, v in (("kcl", 2048.0), ("hc", -31.5), ("pc", -7.0)):
        lin(top(R(name)), top(ROW), 0.0, v)
    lin(top(R("b26")), top(ROW), 0.0, 2.0 ** 26)
    lin(R("pm16"), R("pm"), 1.0, 16.0)
    lin(R("pm4"), R("pm"), 4095.0, 4095.0)
    lin(R("qb"), R("pm"), 32.5)
    lin(R("qb16"), R("pm"), 32.5, 16 * 32.5)
    lin(R("pw2"), R("po"), 128.0 * 16383.0, 128.0)
    lin(R("pw3"), R("po"), -128.0 * 16383.0, -128.0)
    lin(R("gk"), R("po"), 8.0, R("pg"))
    lin(R("gs"), R("gs"), 1.0, 1.0)
    lin(R("bl"), R("sr"), R("pw2"))
    lin(R("br"), R("sl_"), R("pw3"))
    lin(R("two"), ROW, 0.0, 2.0)
    cp(R("wtf"), R("wti"))
    tt(R("ekt"), R("kt"), R("mk2"), A.mult, R("expl"))
    ts(R("bww"), R("row"), R("pe"), R("wtf"), A.is_equal, A.mult)
    mm(R("b7", 0, 256), R("bof"), R("ekt"), True, True)
    lin(R("nid"), R("idb"), -1.0)
    lin(R("kr"), R("b7", 0, 192), 32.0)
    for k in range(8):
        lin(R("th2", k, 512, 8), R("b7", 192, 256), 4096.0, -(2.0 ** 24))
    ts(R("sel"), R("row"), R("pe"), R("s16"), A.is_equal, A.mult)
    ts(R("grp"), R("gi"), R("gk"), R("gs"), A.is_equal, A.mult)
    ts(R("bw"), R("mg"), R("pg"), R("wtf"), A.is_equal, A.mult)
    ts(R("idh"), ROW, R("pf"), None, A.is_equal)
    setrow(top(R("kcl")), 0, -(2.0 ** 24))
    iota(R("zz"), [[0, 128]])
    select(top(R("cr", 0, 128)), top(R("b26")), [[1, 128]], A.is_ge, 0.0, -112, -1)
    iota(top(R("cr", 128, 129)), [[0, 1]])
    mid, own, lhs = (rows(r, 32, 64) for r in (R("cr", 0, 128), R("cr", 128, 129), R("ca")))
    iota(mid, [[0, 128]], 0, 1)
    select(own, rows(R("ones", 0, 1), 32, 64), [[0, 1]], A.is_gt, -(2.0 ** -22), 0, 0)
    for p, v, w in ((32, -(2.0 ** 27), 32.0), (33, 2.0 ** 23, 2.0 ** 24), (34, 0.0, -4096.0)):
        setrow(mid, p, v)
        setrow(own, p, w)
    select(lhs, rows(R("q16"), 32, 64), [[0, 128]], A.is_equal, 1.0, 0, 1)
    select(lhs, lhs, [[0, 128]], A.is_ge, -(2.0 ** 31), 2, -1)
    select(R("omi"), ONE, [[-1, 128]], A.not_equal, 0.0, 0, 1)
    select(R("rneg"), R("zz"), [[0, 8], [1, 16]], A.not_equal, -(2.0 ** 21), 0, 0)
    select(top(R("nm")), top(R("zz")), [[0, 8], [1, 16]], A.is_equal, -(2.0 ** 20), 0, -1)
    iota(top(R("nq")), [[0, 8], [-1, 16]])
    iota(top(R("c31c")), [[0, 8]], 0, 128)
    setrow(top(R("c31c")), 1, -7.5 / 16)
    iota(top(R("io")), [[32, 128]])
    setrow(top(R("io")), 1, 1.0)
    iota(top(R("dl")), [[1, 128]])
    setrow(top(R("dl")), 0, 1.0)
    for k, w in enumerate((1, 16384)):
        iota(top(blk("dr", k)), [[w, 128]])
        setrow(top(blk("dr", k)), 1, -float(w))
    iota(top(R("ac")), [[32, 128]])
    setrow(top(R("ac")), 1, 28672.0)
    setrow(top(R("ac")), 2, -7.0)

    def later_constants():
        for name, scale in (("bo27", 2.0 ** 27), ("bo12", 4096.0), ("boh", 1.0), ("bo", 1.0), ("nbo", -1.0)):
            lin(R(name), R("bof"), scale)
        lin(R("ngrp"), R("grp"), -1.0)
        lin(R("kperm"), R("kperm"), 1.0 / 128.0)
        lin(R("mks"), MK, (1.0 - 2.0 ** -13) / 16.0)
        lin(R("selr"), R("bof"), R("s15"))
        lin(R("b1", 256, 512), R("pl"), 1.0, R("pm"))
        lin(R("b1", 0, 256), R("pl"), 4095.0, R("pm4"))

    extra = []
    ne = len(topo.engines(core, T.cores[(rank + 1) % N]))
    far = [kr for kr in (2, 1, 3) if topo.die(T.cores[(kr + rank) % N]) != topo.die(core)]
    near = [kr for kr in (1, 2, 3) if kr not in far]

    for t in range(3):
        X = "x%d" % t
        Xn = "x%d" % (t + 1)
        ko = "ko%d" % t
        xr = "xr%d" % t
        early = t == 0

        def last(a, st):
            return R(xr, a, 128, st) if t else R(X, 32 * a + 31, 4096, 32 * st)
        for s in range(16):
            mm(R("b4", 0, 8), band("bww", s), last(s, 16), s == 0, s == 15)
        if t == 0:
            act(R(xr, 0, 128), last(0, 1), F.Copy)
        for w in (128, 256, 512):
            act(R(xr, w, 2 * w), R(xr, 0, w), F.Copy)
        e = 8 * LATE
        mm(R("b0", 0, e), rows(R("kcl"), 0, 2), rows(R("ones", 0, e), 0, 2), True, False)
        mm(R("b5", 0, 512 - e), rows(R("kcl"), 0, 2), rows(R("ones", 0, 512 - e), 0, 2), True, False)
        iota(R("wb"), [[0, 264]])
        cp(R("ui"), R("b4", 0, 8))
        ts(R("ub"), R("ui"), 4095, None, A.bitwise_and)
        tt(R("sq"), R("ub"), R("ub"), A.mult)
        ts(R("uf"), R("ub"), -4096.0, None, A.add)
        ts(R("u2"), R("sq"), -15.0, M28, A.add, A.add)
        for k in range(8):
            ts(R("cv", k, 512, 8), blk("kr", t, 64), R("uf", k, k + 1), R("u2", k, k + 1), A.mult, A.add)
        for a, b in ((0, 64), (64, 512)):
            ts(R("ci", a, b), R("cv", a, b), 5, 4095, A.arith_shift_right, A.bitwise_and)
            cp(R("cl", a, b), R("ci", a, b))

        def wide(name, m0, m1):
            return R(name, 128 * m0, 128 * m1)

        def good(bank, a, b):
            tt(R("gd", a, b), R(bank, 0, b - a), R("th2", a, b), A.is_lt)
            tt(R("mk", a, b), R(bank, 0, b - a), R("gd", a, b), A.mult)

        for what, m0, m1 in PLAN:
            d, ab, lst = wide("d", m0, m1), wide("ab", m0, m1), R("cl", 8 * m0, 8 * m1)
            bank = R("b%d" % (6 + m0 // 4 % 2), 0, 128 * (m1 - m0))
            out = R("b5", 8 * (m0 - LATE), 8 * (m1 - LATE)) if m0 >= LATE else R("b0", 8 * m0, 8 * m1)
            if what == "gs":
                act(d, R(X), F.Copy, lst)
            elif what == "sub":
                mm(bank, R("idb"), d, True, False)
                mm(bank, R("nid"), R(xr, 0, 128 * (m1 - m0)), False, True)
            elif what == "abs":
                act(ab, bank, F.Abs)
            elif what == "gv":
                tt(d, R(X), R(xr, 0, 128 * (m1 - m0)), A.subtract, lst)
            elif what == "as":
                act(ab, d, F.Abs)
            elif what == "neg":
                ts(ab, d, 0.0, -2.0, A.min, A.mult)
            elif what in ("d", "ab"):
                for s in range(16):
                    mm(out, band("ldw", s), R(what, 128 * m0 + s, 128 * m1, 16), False, m1 in (LATE, 64) and s == 15)
            elif what == "c16":
                ts(R("c16"), R("cl"), -2048.0, None, A.add)
            elif what == "col":
                mm(out, R("idh"), R("c16", 8 * m0, 8 * m1), False, False)
            elif what == "good":
                good("b5" if m0 else "b0", 8 * m0, 8 * m1)
            else:
                mm(R("b6", 0, 128), rows(R("hc"), 0, 1), rows(ONE, 0, 1), True, False)
                for k in range(4):
                    mm(blk("b6", k, 32), R("bw"), last(k, 4), False, k == 3)
        if t == 0:
            later_constants()
        for bank, js in BANKS:
            mm(R(bank, 0, BANKW[bank]), rows(R("zz"), 0, 1), rows(R("ones", 0, BANKW[bank]), 0, 1), True, False)
        for j in range(8):
            bank, c, w = SEG[j]
            mm(R(bank, c, c + w + 1), rows(R("ca"), 0, 35 + j), rows(R("cr", 128 - w, 129), 0, 35 + j), False, False)
        for k in range(8):
            red(R("best", k, k + 1), R("mk", k, 512, 8), A.min)
        ts(R("jI"), R("best"), 5, 127, A.arith_shift_right, A.bitwise_and)
        ts(R("dio", 0, 8), R("best"), 2.0 ** -12, 2047.5 + 2.0 ** -13, A.mult, A.add)
        ts(R("dio", 8, 16), R("best"), 1, 15, A.arith_shift_right, A.bitwise_and)
        tt(R("ej"), R("jI"), MK, A.mult, E8)
        tt(R("ed"), R("dio"), R("mk2"), A.mult, R("expl"))
        ts(R("hr"), R("b6", 0, 128), M29, -M29, A.add, A.add)
        tt(R("hf"), R("b6", 0, 128), R("hr"), A.subtract)
        lin(blk("b0", 0), R("hf"), R("pm"), R("qb"))
        lin(blk("b0", 1), R("hf"), R("pm16"), R("qb16"))
        seg = {j: R(SEG[j][0], SEG[j][1], SEG[j][1] + SEG[j][2]) for j in range(8)}
        for part, js in (("target", (7, 6, 5, 4)), ("key", (7, 6, 5, 4)), ("target", (3, 2, 1, 0)), ("key", (3, 2, 1, 0))):
            for j in js:
                w = SEG[j][2]
                if part == "target":
                    mm(seg[j], R("bo27"), R("ej", 0, w), False, False)
                    mm(seg[j], rows(ONE, 0, 2), rows(R("io", 0, w), 0, 2), False, False)
                else:
                    mm(seg[j], R("bo12"), R("ed", 0, w), False, False)
                    mm(seg[j], R("boh"), R("ed", 128, 128 + w), False, j in (6, 4, 0))
        for j in range(7, -1, -1):
            red(R("acc", j, j + 1), R(SEG[j][0], SEG[j][1], SEG[j][1] + 1 + SEG[j][2]), A.min, True)
        ts(R("fI"), R("acc"), 5, 127, A.arith_shift_right, A.bitwise_and)
        ts(R("cI"), R("acc"), 31, None, A.bitwise_and)
        tt(R("ef"), R("fI"), MK, A.mult, E8)
        mm(R("b5", 0, 128), R("bo"), R("ef"), True, True)
        cp(R("fl0"), R("fI"))
        act(R("f0"), R("b5", 0, 128), F.Copy)
        tt(R("el"), R("cI"), MK, A.mult, E8)
        mm(R("b4", 0, 128), rows(R("two"), 0, 16), rows(ONE, 0, 16), True, False)
        mm(R("b4", 0, 128), R("nbo"), R("el"), False, True)
        mm(R("b5", 128, 384), R("two"), R("grp"), True, False)
        mm(R("b5", 128, 384), R("el"), R("ngrp"), False, True)
        mm(R("b3", 256, 384), rows(ONE, 0, 3), rows(R("ac"), 0, 3), True, False)
        mm(R("b3", 256, 384), R("bo"), R("el"), False, True)
        for bank, g0, q in DIFF:
            mm(R(bank, 0, 256), rows(R("dl"), 0, 2), rows(R("dr"), 0, 2), True, False)
        begun = fence()
        gaps = [
            lambda: red(R("lc"), R("b4", 0, 128), A.add),
            lambda: ts(R("sk"), R("kperm"), R("lc"), -63.5 / 128.0, A.mult, A.add),
            lambda: tt(R("pp", 0, 256, 2), R("sk"), blk("b0", 0), A.add),
            lambda: tt(R("pp", 1, 256, 2), R("sk"), blk("b0", 1), A.add),
        ]
        for k in range(4):
            fl = R("fl%d" % k)
            tt(R("mm"), R("f%d" % k), MK, A.mult, fl)
            act(R("h%d" % k), R("f%d" % k), F.Copy, fl)
            act(R("f%d" % (k + 1)), R("h%d" % k), F.Copy, fl)
            scan(R("sc"), R("rst"), R("mm"), 0.0, A.mult, A.add)
            gaps[k]()
            cp(R("fl%d" % (k + 1)), R("sc", 15, 128, 16))
        fl = R("fl4")
        act(R("f5"), R("f4"), F.Copy, fl)
        act(R("f6"), R("f5"), F.Copy, fl)
        pos = R("b4", 384, 512)
        mm(pos, rows(R("pc"), 0, 1), rows(ONE, 0, 1), True, False)
        ts(R("b0", 256, 512), R("pp"), R("lc"), R("lc"), A.is_ge, A.mult)
        tt(R("pw"), R("pp"), R("b0", 256, 512), A.subtract)
        if early:
            mm(R("b0", 0, 128), rows(R("nq"), 0, 1), rows(ONE, 0, 1), True, False)
            mm(R("b0", 0, 128), R("selr"), R("pw", 1, 256, 2), False, True)
        ts(R("lf"), R("f6"), R("sl_"), R("bl"), A.mult, A.add, fl)
        act(R("rt"), R("f6"), F.Identity, fl, R("sr"), R("br"))
        act(R("lb"), R("b5", 128, 384), F.Copy)
        begun()
        for bank, g0, q in DIFF:
            p = 16 * g0
            mm(blk(bank, 0), rows(R("lf"), p, p + 16), rows(R("rt"), p, p + 16), False, False)
            mm(blk(bank, 1), rows(R("lf"), p, p + 32), rows(R("rt"), p, p + 32), False, True)
        for k in range(4, 8):
            mm(rows(pos, 32 * (k // 2), 32 * (k // 2) + 32), blk("lb", k, 32), R("omi"), False, False)
        if early:
            ts(R("hr"), R("b0", 0, 128), M27, -M27, A.add, A.add)
        for bank, g0, q in DIFF:
            if q == "V":
                ts(R("cmp", 128 * g0, 128 * g0 + 256), R(bank, 0, 256), 0.0, None, A.is_gt)
            else:
                act(R("cmp", 128 * g0, 128 * g0 + 256), R(bank, 0, 256), F.Sign)
        lin(R("fst"), R("b3", 256, 384), 1.0)
        for bank, g0, q in DIFF:
            for k in (g0, g0 + 1):
                mm(rows(pos, 16 * g0, 16 * g0 + 32), blk("lb", k, 32), blk("cmp", k), False, k > g0)
        if t < 2:
            lin(R("p16"), R("pw", 1, 256, 2), 1.0, -2048.0)
            mm(R("b5", 0, 8), rows(ONE, 0, 2), rows(R("c31c"), 0, 2), True, False)
            for s in range(16):
                mm(R("b5", 0, 8), band("sel", s), R("p16", s, 128, 16), False, s == 15)
        if early:
            tt(R("hf"), R("b0", 0, 128), R("hr"), A.is_equal)
            mm(R("b2", 0, 128), rows(R("ca"), 0, 16), rows(R("nm"), 0, 16), True, False)
        cp(R("plist"), R("pw"))
        tt(R("mp"), pos, R("mks"), A.mult)
        lin(R("t4"), pos, 4095.0)
        scan(R("sp"), R("rst"), R("mp"), 0.0, A.mult, A.add)
        ts(R("celll"), R("sp", 15, 128, 16), M23, -M23, A.add, A.add)
        tt(R("wb", 8, 264), R("t4"), R("fst"), A.add, None, R("celll"))

        def step(n, a, b):
            if n == 0:
                tt(R("b7", a, b), R("wb", 8 + a, 8 + b), R("b1", a, b), A.is_lt)
            elif n == 1:
                tt(R("w1", a, b), R("wb", 8 + a, 8 + b), R("b7", a, b), A.mult)
            elif n == 2:
                scan(R("ff", a, b), R("wb", 7 + a, 7 + b), R("w1", a, b), R("ff", a - 1, a) if a else 0.0, A.max, A.max)
            elif n == 3:
                tt(R("si", a, b), R("ff", a, b), R("b1", 256 + a, 256 + b), A.add)
            elif n == 4:
                ts(R("sj", a, b), R("si", a, b), 4095, None, A.bitwise_and)
            else:
                cp(R("sl", a, b), R("sj", a, b))
        cut = LAYS[t]
        for n, second in ((0, 0), (0, 1), (1, 0), (1, 1), (2, 0), (3, 0), (2, 1), (4, 0), (3, 1), (5, 0), (4, 1)):
            if second:
                step(n, cut, 256)
            else:
                step(n, 0, cut)
            if n == 5 and early:
                ts(R("c31"), R("b5", 0, 8), M23, -M23, A.add, A.add)
        mine = cut - FILL if early else cut
        act(R("lay", 0, 16 * mine), R(X), F.Copy, R("sl", 0, mine))

        def kids(q, kr, a, b):
            buf, o = (ko, MB * (kr - 1)) if kr else (Xn, MB * rank)
            lst = R("plist", 64 * kr + a, 64 * kr + b)
            if q == "V":
                cp(R(buf, o + 16 * a, o + 16 * b), R("lay"), lst)
            else:
                act(R(buf, o + 16 * a, o + 16 * b), R("lay"), F.Copy, lst)

        def send(pieces, into, rs, ls):
            sync("G", [], [buf for kr, buf in pieces])
            n = ne if len(pieces) == 1 else ne // 4
            calls = []
            for k, (kr, buf) in enumerate(pieces):
                dst = T.cores[(kr + rank) % N]
                mask = sum(1 << x for x in topo.engines(core, dst)[n * k:n * k + n])
                calls.append(RemoteDMATransfer(dst_ids=[DstId(rid=topo.addr(dst)[0], pnc=topo.addr(dst)[1])],
                                               dma_engine_mask=mask, srcs=[ap(buf)], dsts=[ap(into)], remote_sem=T.sem[rs]))
            g.remote_dma_fused(calls, local_sem=T.sem[ls])

        def ahead(window):
            lo, xn = "lo%d" % t, "xr%d" % (t + 1)
            cp(R(lo, 32, 128), window, R("l31", 2, 8))
            send([(kr, blk(lo, kr, 32)) for kr in (1, 2, 3)], blk(xn, rank, 32), "sm%d" % t, "lq%d" % t)
            cp(blk(xn, rank, 32), window, R("l31", 0, 2))
            arrive("sm%d" % t, 3 * (ne // 4), [blk(xn, r, 32) for r in range(N) if r != rank])
            extra.append(("lq%d" % t, 3 * (ne // 4)))
        if early:
            tt(R("vrow"), R("sj"), R("hf"), A.mult, R("c31"))
            mm(R("b2", 0, 128), R("bof"), R("vrow"), False, True)
            step(5, cut, 256)
            cp(R("lay", 16 * mine, 16 * cut), R(X), R("sl", mine, cut))
            scan(R("sp"), R("rneg"), R("b2", 0, 128), 0.0, A.add, A.max)
            cp(R("l31"), R("sp", 15, 128, 16))
            ahead(R(X))
        else:
            step(5, cut, 256)
            if t < 2:
                ts(R("l31"), R("b5", 0, 8), 16.0, 7.5, A.mult, A.add)
        cp(R("lay", 16 * cut, 4096), R(X), R("sl", cut, 256))
        if t < 2 and not early:
            ahead(R("lay"))
        order = far + near + [0]
        landed = []
        for n, (k, a, m, b) in enumerate(KIDS[t]):
            kr = order[k]
            if m > a:
                kids("V", kr, a, m)
            kids("S", kr, m, b)
            if kr:
                o = MB * (kr - 1)
                send([(kr, R(ko, o + 16 * a, o + 16 * b))], R(Xn, MB * rank + 16 * a, MB * rank + 16 * b),
                     "ar%d_%d" % (t, n), "ls%d" % t)
            s = (rank + kr) % N
            landed.append((k, R(Xn, MB * s + 16 * a, MB * s + 16 * b)))
        for n, (k, r) in enumerate(landed):
            if k < 3:
                arrive("ar%d_%d" % (t, n), ne, [r])
        extra.append(("ls%d" % t, ne * sum(k < 3 for k, r in landed)))
    for k, r in landed:
        dma("Y" if k < 3 else "S", T.y[:, r[1]:r[2]], ap(r), [], [r])
    finish(extra)
